import numpy as np
import ml_dtypes


def mxq(x, axis, fmt="e4m3"):
    dtype, down = {"e4m3": (ml_dtypes.float8_e4m3fn, 7), "e5m2": (ml_dtypes.float8_e5m2, 14)}[fmt]
    v = np.moveaxis(np.asarray(x, np.float32).astype(ml_dtypes.bfloat16).astype(np.float64), axis, -1)
    blocks = v.reshape(v.shape[:-1] + (-1, 32))
    amax = np.abs(blocks).max(-1, keepdims=True)
    byte = np.maximum(np.where(amax > 0, np.frexp(amax)[1] - 1 + 127, 0) - down, 1)
    scale = np.exp2(byte - 127.0)
    codes = (blocks / scale).astype(np.float32).astype(dtype).astype(np.float64)
    return np.moveaxis((codes * scale).reshape(v.shape), -1, axis)


WIDE = False


def mx_kscale(k):
    if not WIDE:
        return np.ones(k)
    levels = np.array([10, -10, 5, -5, 0])
    if k % 512:
        return np.exp2(np.random.permutation(np.resize(levels, k // 32))).repeat(32)
    a = np.empty((k // 512, 16))
    for p in range(k // 512):
        a[p, :8] = np.random.permutation(np.resize(levels, 8))
        for g in range(8):
            far = levels[np.abs(levels - a[p, g]) >= 10]
            a[p, g + 8] = far[np.random.randint(len(far))]
    return np.exp2(a.ravel()).repeat(32)


def f64(x):
    return np.asarray(x).astype(np.float64)


def striped(idx):
    return np.tile(idx.reshape(-1, 16).T, (8, 1)).astype(np.uint16)


def unstriped(offs):
    return offs[:16].T.reshape(-1).astype(np.int64)


E2M1 = np.array([0.0, 0.5, 1.0, 1.5, 2.0, 3.0, 4.0, 6.0, -0.0, -0.5, -1.0, -1.5, -2.0, -3.0, -4.0, -6.0])


def pack_weight(w, fmt):
    k, n = w.shape
    w = f64(np.asarray(w, np.float32).astype(ml_dtypes.bfloat16)).reshape(k // 32, 32, n)
    amax = np.abs(w).max(1)
    if fmt == "e4m3":
        byte = np.frexp(amax)[1] - 1 + 127 - 7
    else:
        mant, ex = np.frexp(amax / 6.0)
        byte = np.where(mant > 0.5, ex, ex - 1) + 127
    byte = np.clip(np.where(amax > 0, byte, 1), 1, 254)
    scaled = (w * np.exp2(127.0 - byte)[:, None, :]).reshape(k, n).astype(np.float32)
    by_word = np.ascontiguousarray(scaled.reshape(k // 512, 128, 4, n).transpose(0, 1, 3, 2))
    if fmt == "e4m3":
        words = by_word.astype(ml_dtypes.float8_e4m3fn).view(np.uint8)
    else:
        c = by_word.astype(ml_dtypes.float4_e2m1fn).view(np.uint8) & 0xF
        words = (c[..., 0::2] | (c[..., 1::2] << 4)).reshape(k // 512, 128, 2 * n)
    return np.ascontiguousarray(words), np.ascontiguousarray(byte.astype(np.uint8).reshape(k // 512, 16, n))


def unpack_weight(words, scales, fmt):
    g, _, n = scales.shape
    words = np.ascontiguousarray(words).reshape(g, 128, n, -1)
    if fmt == "e4m3":
        vals = words.view(ml_dtypes.float8_e4m3fn).astype(np.float64)
    else:
        nib = np.empty((g, 128, n, 4), np.uint8)
        nib[..., 0::2] = words & 0xF
        nib[..., 1::2] = words >> 4
        vals = E2M1[nib]
    vals = vals * np.repeat(np.exp2(scales.astype(np.float64) - 127.0), 8, axis=1)[..., None]
    return vals.transpose(0, 1, 3, 2).reshape(g * 512, n)


def gelu(v):
    return 0.5 * v * (1.0 + np.tanh(np.sqrt(2.0 / np.pi) * (v + 0.044715 * v**3)))


K, T, S, H, N = 1024, 4096, 1024, 512, 256

def setup_inputs():
    n = np.random.standard_normal
    s = mx_kscale(K)[:, None]
    u = mx_kscale(H)[:, None]
    tab_words, tab_scales = pack_weight(n((K, T)) * s, "e4m3")
    wr_words, wr_scales = pack_weight(n((K, H)) / np.sqrt(K) / s, "e2m1")
    wv_words, wv_scales = pack_weight(n((K, H)) / np.sqrt(K) / s, "e4m3")
    return {
        "tab_words": tab_words, "tab_scales": tab_scales,
        "offs": striped(np.random.permutation(T)[:S]),
        "we": (n((K, H)) / np.sqrt(K) / s * u.T).astype(np.float32),
        "wr_words": wr_words, "wr_scales": wr_scales,
        "wv_words": wv_words, "wv_scales": wv_scales,
        "wa": (n((H, N)) / np.sqrt(H) / u).astype(np.float32),
    }

def reference(tab_words, tab_scales, offs, we, wr_words, wr_scales, wv_words, wv_scales, wa):
    v = unpack_weight(tab_words, tab_scales, "e4m3")[:, unstriped(offs)]
    weq = mxq(f64(we), 0, "e4m3")
    wr = unpack_weight(wr_words, wr_scales, "e2m1")
    wv = unpack_weight(wv_words, wv_scales, "e4m3")
    e = weq.T @ v
    m = wr.T @ v
    c = wv.T @ v
    h = e * m / np.sqrt(1.0 + np.square(c))
    hq = mxq(h, 0, "e4m3")
    waq = mxq(f64(wa), 0, "e4m3")
    return waq.T @ hq

@@ -1,0 +1,251 @@
+from contextlib import ExitStack
+
+import concourse.mybir as mybir
+
+K, T, S, H, N = 1024, 4096, 1024, 512, 256
+FLOPS = 2 * 3 * K * H * S + 2 * H * N * S
+
+F32 = mybir.dt.float32
+BF16 = mybir.dt.bfloat16
+I32 = mybir.dt.int32
+U32 = mybir.dt.uint32
+U16 = mybir.dt.uint16
+U8 = mybir.dt.uint8
+FP8X4 = mybir.dt.float8_e4m3fn_x4
+FP4X4 = mybir.dt.float4_e2m1fn_x4
+ACT = mybir.ActivationFunctionType
+ALU = mybir.AluOpType
+
+P = 128
+PASSES = 2
+HALF = 512
+TOK = 128
+CAST_ENGINES = [["g","g","g","g"],["g","g","s","v"]]
+WA_ENGINE = "g"
+
+
+def tile_list_factor_risk_allocation_kernel(
+    tc, tab_words, tab_scales, offs, we, wr_words, wr_scales, wv_words, wv_scales, wa, out
+):
+    nc = tc.nc
+
+    def cast(engine, dst, src):
+        if engine == "g":
+            nc.gpsimd.tensor_scalar(out=dst, in0=src, scalar1=1.0, scalar2=0.0, op0=ALU.mult, op1=ALU.add)
+        elif engine == "s":
+            nc.scalar.copy(out=dst, in_=src)
+        else:
+            nc.vector.tensor_copy(out=dst, in_=src)
+
+    with ExitStack() as ctx:
+        keep = ctx.enter_context(tc.tile_pool(name="keep", bufs=1))
+        work = ctx.enter_context(tc.tile_pool(name="work", bufs=3))
+        psum = ctx.enter_context(tc.psum_pool(name="psum", bufs=1))
+
+        offsets = keep.tile([P, S // 16], U16, name="offsets")
+        nc.sync.dma_start(offsets[:], offs)
+
+        warm = keep.tile([P, 2], F32, name="warm")
+        nc.vector.memset(warm[:, 0:1], 1.0)
+        nc.scalar.activation(out=warm[:, 1:2], in_=warm[:, 0:1], func=ACT.Abs_reciprocal_sqrt)
+
+        tsc = keep.tile([P, T // 4], I32, name="tsc", align_bytes=64)
+        nc.sync.dma_start(tsc[0:32, :], tab_scales.rearrange("a q t -> q a t").bitcast(I32))
+        nc.gpsimd.memset(tsc[32:64, :], 0)
+        nc.vector.memset(tsc[64:128, :], 0)
+        wsc_r = keep.tile([32, H // 4], I32, name="wsc_r", align_bytes=64)
+        wsc_v = keep.tile([32, H // 4], I32, name="wsc_v", align_bytes=64)
+        nc.sync.dma_start(wsc_v[:], wv_scales.rearrange("a q y -> q a y").bitcast(I32))
+        nc.sync.dma_start(wsc_r[:], wr_scales.rearrange("a q y -> q a y").bitcast(I32))
+
+        tab0 = keep.tile([P, T], I32, name="tab0", tag="first", align_bytes=64)
+        wv_raw = keep.tile([P, PASSES, H], I32, name="wv_raw", align_bytes=64)
+        nc.sync.dma_start(tab0[:], tab_words[0].rearrange("p t i -> p (t i)").bitcast(I32))
+        nc.sync.dma_start(wv_raw[:], wv_words.rearrange("a p y i -> p a (y i)").bitcast(I32))
+
+        PW = (S + 2 * H) // 4
+        planes = keep.tile([P, PASSES, PW], I32, name="planes", align_bytes=64)
+        nc.vector.memset(planes[:], 0)
+        sg = keep.tile([P, S], U8, name="sg", tag="second", align_bytes=64)
+        nc.vector.tensor_copy(sg[:], tsc[:].bitcast(U8).indirect(offsets[:]))
+        stage = keep.tile([32, PW], I32, name="stage", tag="third", align_bytes=64)
+        for src, lo in ((wsc_v, S // 4), (wsc_r, (S + H) // 4)):
+            nc.vector.tensor_copy(
+                out=stage[:, lo : lo + H // 4].rearrange("p (t g i) -> p t g i", t=4, i=2),
+                in_=src[:].rearrange("p (g t i) -> p t g i", t=4, i=2),
+            )
+        nc.vector.tensor_copy(out=stage[:, 0 : S // 4], in_=sg[0:32, :].bitcast(I32))
+        for q in range(4):
+            nc.sync.dma_start(planes[32 * q : 32 * q + 4, :, :], stage[8 * q : 8 * q + 8, :])
+        tab1 = keep.tile([P, T], I32, name="tab1", tag="second", align_bytes=64)
+        nc.sync.dma_start(tab1[:], tab_words[1].rearrange("p t i -> p (t i)").bitcast(I32))
+        wr_raw = keep.tile([P, PASSES, H // 2], I32, name="wr_raw", tag="third", align_bytes=64)
+        nc.sync.dma_start(wr_raw[:], wr_words.rearrange("a p y -> p a y").bitcast(I32))
+        planes8 = planes[:].bitcast(U8)
+
+        def v_scale(a, lo, n):
+            return planes8[:, a, lo : lo + n]
+
+        def wv_scale(a, t):
+            return planes8[:, a, S + P * t : S + P * (t + 1)]
+
+        def wr_scale(a, t):
+            return planes8[:, a, S + H + P * t : S + H + P * (t + 1)]
+
+        vq = [[keep.tile([P, HALF], U32, name="vq%d%d" % (a, b), align_bytes=64) for b in range(2)] for a in range(PASSES)]
+
+        def gather(a, b):
+            win = (tab0[:], tab1[:])[a]
+            nc.vector.tensor_copy(vq[a][b][:], win.bitcast(U32).indirect(offsets[:, 32 * b : 32 * (b + 1)]))
+
+        wv_q = keep.tile([P, PASSES, H], I32, name="wv_q", align_bytes=64)
+        wr_q = keep.tile([P, PASSES, H // 2], I32, name="wr_q", align_bytes=64)
+
+        def permute(dst, src, run):
+            for a in range(PASSES):
+                nc.vector.tensor_copy(
+                    out=dst[:, a, :].rearrange("p (t g i) -> p t g i", t=4, i=run),
+                    in_=src[:, a, :].rearrange("p (g t i) -> p t g i", t=4, i=run),
+                )
+
+        def c_pass(acc, a, b, t):
+            nc.tensor.matmul_mx(
+                out=acc[:], lhsT=wv_q[:, a, P * t : P * (t + 1)].bitcast(FP8X4), lhsT_scale=wv_scale(a, t),
+                rhs=vq[a][b][:].bitcast(FP8X4), rhs_scale=v_scale(a, HALF * b, HALF), start=(a == 0), stop=(a == 1),
+            )
+
+        def m_pass(acc, a, b, t):
+            nc.tensor.matmul_mx(
+                out=acc[:], lhsT=wr_q[:, a, 64 * t : 64 * (t + 1)].bitcast(U8).bitcast(FP4X4), lhsT_scale=wr_scale(a, t),
+                rhs=vq[a][b][:].bitcast(FP8X4), rhs_scale=v_scale(a, HALF * b, HALF), start=(a == 0), stop=(a == 1),
+            )
+
+        gather(0, 0)
+        gather(0, 1)
+        permute(wv_q, wv_raw, 8)
+
+        late = keep.tile([P, 5 * 1024], F32, name="late", tag="first", align_bytes=64)
+        we_raw = late[:, 0:4096].rearrange("p (a j r) -> p a j r", a=2, j=4)
+        wa_raw = late[:, 4096:5120].rearrange("p (t n) -> p t n", t=4)
+        for a in range(PASSES):
+            nc.sync.dma_start(we_raw[:, a], we[512 * a : 512 * (a + 1), :].rearrange("(p j) r -> p j r", j=4))
+        wa_rows = wa.rearrange("(g t i) n -> t g i n", t=4, i=8)
+        for t in range(4):
+            nc.sync.dma_start(wa_raw[:, t, :], wa_rows[t])
+
+        c_acc = [[psum.tile([P, HALF], F32, name="c%d%d" % (b, t), tag="bank%d" % (4 * b + t)) for t in range(4)] for b in range(2)]
+        for b in range(2):
+            for t in range(4):
+                c_pass(c_acc[b][t], 0, b, t)
+        gather(1, 0)
+        gather(1, 1)
+        permute(wr_q, wr_raw, 4)
+        for b in range(2):
+            for t in range(4):
+                c_pass(c_acc[b][t], 1, b, t)
+
+        damp = [keep.tile([P, 4, HALF], F32, name="damp%d" % b, align_bytes=64) for b in range(2)]
+        md = [keep.tile([P, 4, HALF], F32, name="md%d" % b, align_bytes=64) for b in range(2)]
+        we_bf = [keep.tile([P, 4, P, 4], BF16, name="we_bf%d" % a, align_bytes=64) for a in range(PASSES)]
+        we_q = keep.tile([P, PASSES, H], U32, name="we_q", align_bytes=64)
+        we_s = keep.tile([P, PASSES, H], U8, name="we_s", align_bytes=64)
+        wa_bf = keep.tile([P, N, 4], BF16, name="wa_bf", align_bytes=64)
+        wa_q = keep.tile([P, N], U32, name="wa_q", align_bytes=64)
+        wa_s = keep.tile([P, N], U8, name="wa_s", align_bytes=64)
+
+        def damping(b, t):
+            sq = work.tile([P, HALF], F32, name="sq", align_bytes=64)
+            nc.scalar.activation(out=sq[:], in_=c_acc[b][t][:], func=ACT.Square)
+            nc.scalar.activation(out=damp[b][:, t, :], in_=sq[:], func=ACT.Abs_reciprocal_sqrt, bias=1.0)
+
+        def forecast(b, t, bank):
+            acc = psum.tile([P, HALF], F32, name="m", tag="bank%d" % bank)
+            for a in range(PASSES):
+                m_pass(acc, a, b, t)
+            nc.vector.tensor_tensor(out=md[b][:, t, :], in0=acc[:], in1=damp[b][:, t, :], op=ALU.mult)
+
+        def cast_we(a):
+            for t in range(4):
+                cast(
+                    CAST_ENGINES[a][t],
+                    we_bf[a][:, t].rearrange("p (g i) j -> p g i j", i=8),
+                    we_raw[:, a].rearrange("p j (g t i) -> p t g i j", t=4, i=8)[:, t],
+                )
+
+        def quant_we(a):
+            nc.vector.quantize_mx(
+                out=we_q[:, a, :].bitcast(FP8X4), scales=we_s[:, a, :],
+                in_=we_bf[a][:].rearrange("p t c j -> p (t c j)"),
+            )
+
+        h_bf = keep.tile([P, S, 4], BF16, name="h_bf", align_bytes=64)
+        h_q = keep.tile([P, S], U32, name="h_q", align_bytes=64)
+        h_s = keep.tile([P, S], U8, name="h_s", align_bytes=64)
+        out_v = out.rearrange("(u p) j -> p u j", p=P)
+
+        def exposure(s, bank):
+            b, lo = divmod(TOK * s, HALF)
+            acc = psum.tile([P, 4, TOK], F32, name="e", tag="bank%d" % bank)
+            for t in range(4):
+                for a in range(PASSES):
+                    nc.tensor.matmul_mx(
+                        out=acc[:, t, :], lhsT=we_q[:, a, P * t : P * (t + 1)].bitcast(FP8X4),
+                        lhsT_scale=we_s[:, a, P * t : P * (t + 1)],
+                        rhs=vq[a][b][:, lo : lo + TOK].bitcast(FP8X4), rhs_scale=v_scale(a, TOK * s, TOK),
+                        start=(a == 0), stop=(a == 1),
+                    )
+            nc.vector.tensor_tensor(
+                out=h_bf[:, TOK * s : TOK * (s + 1), :].rearrange("p (c i) t -> p c t i", i=4),
+                in0=acc[:].rearrange("p t (c i) -> p c t i", i=4),
+                in1=md[b][:, :, lo : lo + TOK].rearrange("p t (c i) -> p c t i", i=4),
+                op=ALU.mult,
+            )
+
+        def allocate(group, bank):
+            lo, width = TOK * group[0], TOK * len(group)
+            cols = slice(lo, lo + width)
+            nc.vector.quantize_mx(
+                out=h_q[:, cols].bitcast(FP8X4), scales=h_s[:, cols],
+                in_=h_bf[:, cols, :].rearrange("p n t -> p (n t)"),
+            )
+            acc = psum.tile([P, 2, width], F32, name="o", tag="bank%d" % bank)
+            for u in range(2):
+                nc.tensor.matmul_mx(
+                    out=acc[:, u, :], lhsT=wa_q[:, P * u : P * (u + 1)].bitcast(FP8X4),
+                    lhsT_scale=wa_s[:, P * u : P * (u + 1)],
+                    rhs=h_q[:, cols].bitcast(FP8X4), rhs_scale=h_s[:, cols], start=True, stop=True,
+                )
+            res = work.tile([P, 2, width], F32, name="res", tag="res", bufs=5, align_bytes=64)
+            nc.scalar.copy(out=res[:], in_=acc[:])
+            nc.sync.dma_start(out_v[:, :, cols], res[:])
+
+        for t in range(4):
+            damping(0, t)
+            forecast(0, t, t)
+        cast_we(0)
+        quant_we(0)
+        cast_we(1)
+        quant_we(1)
+        cast(WA_ENGINE, wa_bf[:], wa_raw.rearrange("p t n -> p n t"))
+        damping(1, 0)
+        forecast(1, 0, 0)
+        exposure(0, 1)
+        damping(1, 1)
+        exposure(1, 2)
+        forecast(1, 1, 3)
+        nc.vector.quantize_mx(out=wa_q[:].bitcast(FP8X4), scales=wa_s[:], in_=wa_bf[:].rearrange("p n t -> p (n t)"))
+        damping(1, 2)
+        exposure(2, 4)
+        forecast(1, 2, 0)
+        damping(1, 3)
+        exposure(3, 5)
+        forecast(1, 3, 1)
+        allocate([0, 1], 2)
+        exposure(4, 6)
+        allocate([2, 3], 4)
+        exposure(5, 3)
+        exposure(6, 7)
+        allocate([4, 5], 5)
+        exposure(7, 0)
+        allocate([6], 1)
+        allocate([7], 2)

@@ -20,8 +20,8 @@ P = 128
 PASSES = 2
 HALF = 512
 TOK = 128
-CAST_ENGINES = [["g","g","g","g"],["g","g","s","v"]]
-WA_ENGINE = "g"
+CAST_ENGINES = [["v","v","v","v"],["s","s","v","v"]]
+WA_ENGINE = "s"
 
 
 def tile_list_factor_risk_allocation_kernel(
@@ -50,11 +50,11 @@ def tile_list_factor_risk_allocation_kernel(
         nc.scalar.activation(out=warm[:, 1:2], in_=warm[:, 0:1], func=ACT.Abs_reciprocal_sqrt)
 
         tsc = keep.tile([P, T // 4], I32, name="tsc", align_bytes=64)
-        nc.sync.dma_start(tsc[0:32, :], tab_scales.rearrange("a q t -> q a t").bitcast(I32))
-        nc.gpsimd.memset(tsc[32:64, :], 0)
+        nc.vector.memset(tsc[32:64, :], 0)
         nc.vector.memset(tsc[64:128, :], 0)
         wsc_r = keep.tile([32, H // 4], I32, name="wsc_r", align_bytes=64)
         wsc_v = keep.tile([32, H // 4], I32, name="wsc_v", align_bytes=64)
+        nc.sync.dma_start(tsc[0:32, :], tab_scales.rearrange("a q t -> q a t").bitcast(I32))
         nc.sync.dma_start(wsc_v[:], wv_scales.rearrange("a q y -> q a y").bitcast(I32))
         nc.sync.dma_start(wsc_r[:], wr_scales.rearrange("a q y -> q a y").bitcast(I32))
 
@@ -65,14 +65,14 @@ def tile_list_factor_risk_allocation_kernel(
 
         PW = (S + 2 * H) // 4
         planes = keep.tile([P, PASSES, PW], I32, name="planes", align_bytes=64)
-        nc.vector.memset(planes[:], 0)
+        nc.gpsimd.memset(planes[:], 0)
         sg = keep.tile([P, S], U8, name="sg", tag="second", align_bytes=64)
         nc.vector.tensor_copy(sg[:], tsc[:].bitcast(U8).indirect(offsets[:]))
         stage = keep.tile([32, PW], I32, name="stage", tag="third", align_bytes=64)
         for src, lo in ((wsc_v, S // 4), (wsc_r, (S + H) // 4)):
             nc.vector.tensor_copy(
-                out=stage[:, lo : lo + H // 4].rearrange("p (t g i) -> p t g i", t=4, i=2),
-                in_=src[:].rearrange("p (g t i) -> p t g i", t=4, i=2),
+                out=stage[:, lo : lo + H // 4].rearrange("p (t c k) -> p c t k", t=4, k=4),
+                in_=src[:].rearrange("p (c k t) -> p c t k", t=4, k=4),
             )
         nc.vector.tensor_copy(out=stage[:, 0 : S // 4], in_=sg[0:32, :].bitcast(I32))
         for q in range(4):
@@ -122,14 +122,14 @@ def tile_list_factor_risk_allocation_kernel(
 
         gather(0, 0)
         gather(0, 1)
-        permute(wv_q, wv_raw, 8)
+        permute(wv_q, wv_raw, 4)
 
         late = keep.tile([P, 5 * 1024], F32, name="late", tag="first", align_bytes=64)
         we_raw = late[:, 0:4096].rearrange("p (a j r) -> p a j r", a=2, j=4)
         wa_raw = late[:, 4096:5120].rearrange("p (t n) -> p t n", t=4)
         for a in range(PASSES):
             nc.sync.dma_start(we_raw[:, a], we[512 * a : 512 * (a + 1), :].rearrange("(p j) r -> p j r", j=4))
-        wa_rows = wa.rearrange("(g t i) n -> t g i n", t=4, i=8)
+        wa_rows = wa.rearrange("(g t i) n -> t g i n", t=4, i=4)
         for t in range(4):
             nc.sync.dma_start(wa_raw[:, t, :], wa_rows[t])
 
@@ -139,7 +139,10 @@ def tile_list_factor_risk_allocation_kernel(
                 c_pass(c_acc[b][t], 0, b, t)
         gather(1, 0)
         gather(1, 1)
-        permute(wr_q, wr_raw, 4)
+        nc.vector.tensor_copy(
+            out=wr_q[:].rearrange("p a (t g i) -> p a t g i", t=4, i=2),
+            in_=wr_raw[:].rearrange("p a (g t i) -> p a t g i", t=4, i=2),
+        )
         for b in range(2):
             for t in range(4):
                 c_pass(c_acc[b][t], 1, b, t)
@@ -166,11 +169,13 @@ def tile_list_factor_risk_allocation_kernel(
 
         def cast_we(a):
             for t in range(4):
-                cast(
-                    CAST_ENGINES[a][t],
-                    we_bf[a][:, t].rearrange("p (g i) j -> p g i j", i=8),
-                    we_raw[:, a].rearrange("p j (g t i) -> p t g i j", t=4, i=8)[:, t],
-                )
+                dst = we_bf[a][:, t].rearrange("p (g u e) j -> p g u j e", u=2, e=2)
+                src = we_raw[:, a].rearrange("p j (g t u e) -> p t g u j e", t=4, u=2, e=2)[:, t]
+                if CAST_ENGINES[a][t] == "v":
+                    cast("v", dst, src)
+                else:
+                    for u in range(2):
+                        cast(CAST_ENGINES[a][t], dst[:, :, u], src[:, :, u])
 
         def quant_we(a):
             nc.vector.quantize_mx(
@@ -195,9 +200,9 @@ def tile_list_factor_risk_allocation_kernel(
                         start=(a == 0), stop=(a == 1),
                     )
             nc.vector.tensor_tensor(
-                out=h_bf[:, TOK * s : TOK * (s + 1), :].rearrange("p (c i) t -> p c t i", i=4),
-                in0=acc[:].rearrange("p t (c i) -> p c t i", i=4),
-                in1=md[b][:, :, lo : lo + TOK].rearrange("p t (c i) -> p c t i", i=4),
+                out=h_bf[:, TOK * s : TOK * (s + 1), :].rearrange("p (c i) t -> p c t i", i=2),
+                in0=acc[:].rearrange("p t (c i) -> p c t i", i=2),
+                in1=md[b][:, :, lo : lo + TOK].rearrange("p t (c i) -> p c t i", i=2),
                 op=ALU.mult,
             )
 
@@ -219,30 +224,35 @@ def tile_list_factor_risk_allocation_kernel(
             nc.scalar.copy(out=res[:], in_=acc[:])
             nc.sync.dma_start(out_v[:, :, cols], res[:])
 
-        for t in range(4):
-            damping(0, t)
-            forecast(0, t, t)
+        damping(0, 0)
+        damping(0, 1)
         cast_we(0)
+        damping(0, 2)
+        forecast(0, 0, 0)
         quant_we(0)
+        forecast(0, 1, 1)
         cast_we(1)
+        damping(0, 3)
         quant_we(1)
-        cast(WA_ENGINE, wa_bf[:], wa_raw.rearrange("p t n -> p n t"))
+        forecast(0, 2, 2)
+        forecast(0, 3, 3)
         damping(1, 0)
-        forecast(1, 0, 0)
-        exposure(0, 1)
+        exposure(0, 0)
         damping(1, 1)
-        exposure(1, 2)
-        forecast(1, 1, 3)
+        exposure(1, 1)
+        cast(WA_ENGINE, wa_bf[:].rearrange("p (c i) t -> p c t i", i=2), wa_raw.rearrange("p t (c i) -> p c t i", i=2))
+        forecast(1, 0, 4)
+        exposure(2, 2)
         nc.vector.quantize_mx(out=wa_q[:].bitcast(FP8X4), scales=wa_s[:], in_=wa_bf[:].rearrange("p n t -> p (n t)"))
+        forecast(1, 1, 3)
         damping(1, 2)
-        exposure(2, 4)
-        forecast(1, 2, 0)
-        damping(1, 3)
         exposure(3, 5)
-        forecast(1, 3, 1)
+        damping(1, 3)
+        forecast(1, 2, 0)
         allocate([0, 1], 2)
-        exposure(4, 6)
-        allocate([2, 3], 4)
+        forecast(1, 3, 1)
+        exposure(4, 4)
+        allocate([2, 3], 6)
         exposure(5, 3)
         exposure(6, 7)
         allocate([4, 5], 5)

@@ -75,7 +75,7 @@ def tile_list_factor_risk_allocation_kernel(
                 in_=src[:].rearrange("p (c k t) -> p c t k", t=4, k=4),
             )
         nc.vector.tensor_copy(out=stage[:, 0 : S // 4], in_=sg[0:32, :].bitcast(I32))
-        for q in range(4):
+        for q in (0, 2, 1, 3):
             nc.sync.dma_start(planes[32 * q : 32 * q + 4, :, :], stage[8 * q : 8 * q + 8, :])
         tab1 = keep.tile([P, T], I32, name="tab1", tag="second", align_bytes=64)
         nc.sync.dma_start(tab1[:], tab_words[1].rearrange("p t i -> p (t i)").bitcast(I32))

@@ -171,11 +171,7 @@ def tile_list_factor_risk_allocation_kernel(
             for t in range(4):
                 dst = we_bf[a][:, t].rearrange("p (g u e) j -> p g u j e", u=2, e=2)
                 src = we_raw[:, a].rearrange("p j (g t u e) -> p t g u j e", t=4, u=2, e=2)[:, t]
-                if CAST_ENGINES[a][t] == "v":
-                    cast("v", dst, src)
-                else:
-                    for u in range(2):
-                        cast(CAST_ENGINES[a][t], dst[:, :, u], src[:, :, u])
+                cast(CAST_ENGINES[a][t], dst, src)
 
         def quant_we(a):
             nc.vector.quantize_mx(
@@ -200,9 +196,9 @@ def tile_list_factor_risk_allocation_kernel(
                         start=(a == 0), stop=(a == 1),
                     )
             nc.vector.tensor_tensor(
-                out=h_bf[:, TOK * s : TOK * (s + 1), :].rearrange("p (c i) t -> p c t i", i=2),
-                in0=acc[:].rearrange("p t (c i) -> p c t i", i=2),
-                in1=md[b][:, :, lo : lo + TOK].rearrange("p t (c i) -> p c t i", i=2),
+                out=h_bf[:, TOK * s : TOK * (s + 1), :].rearrange("p (c i) t -> p c t i", i=4),
+                in0=acc[:].rearrange("p t (c i) -> p c t i", i=4),
+                in1=md[b][:, :, lo : lo + TOK].rearrange("p t (c i) -> p c t i", i=4),
                 op=ALU.mult,
             )
 
@@ -227,35 +223,26 @@ def tile_list_factor_risk_allocation_kernel(
         damping(0, 0)
         damping(0, 1)
         cast_we(0)
-        damping(0, 2)
         forecast(0, 0, 0)
         quant_we(0)
         forecast(0, 1, 1)
         cast_we(1)
-        damping(0, 3)
         quant_we(1)
-        forecast(0, 2, 2)
-        forecast(0, 3, 3)
-        damping(1, 0)
-        exposure(0, 0)
-        damping(1, 1)
-        exposure(1, 1)
+        for t in (2, 3):
+            damping(0, t)
+            forecast(0, t, t)
+        for t in range(4):
+            damping(1, t)
+            exposure(t, t)
+            forecast(1, t, 4 + t)
         cast(WA_ENGINE, wa_bf[:].rearrange("p (c i) t -> p c t i", i=2), wa_raw.rearrange("p t (c i) -> p c t i", i=2))
-        forecast(1, 0, 4)
-        exposure(2, 2)
         nc.vector.quantize_mx(out=wa_q[:].bitcast(FP8X4), scales=wa_s[:], in_=wa_bf[:].rearrange("p n t -> p (n t)"))
-        forecast(1, 1, 3)
-        damping(1, 2)
-        exposure(3, 5)
-        damping(1, 3)
-        forecast(1, 2, 0)
-        allocate([0, 1], 2)
-        forecast(1, 3, 1)
-        exposure(4, 4)
-        allocate([2, 3], 6)
-        exposure(5, 3)
-        exposure(6, 7)
-        allocate([4, 5], 5)
-        exposure(7, 0)
-        allocate([6], 1)
-        allocate([7], 2)
+        exposure(4, 0)
+        allocate([0, 1], 4)
+        exposure(5, 1)
+        allocate([2, 3], 5)
+        exposure(6, 2)
+        allocate([4, 5], 6)
+        exposure(7, 3)
+        allocate([6], 7)
+        allocate([7], 4)

@@ -20,8 +20,7 @@ P = 128
 PASSES = 2
 HALF = 512
 TOK = 128
-CAST_ENGINES = [["v","v","v","v"],["s","s","v","v"]]
-WA_ENGINE = "s"
+KIB = 1024
 
 
 def tile_list_factor_risk_allocation_kernel(
@@ -29,16 +28,9 @@ def tile_list_factor_risk_allocation_kernel(
 ):
     nc = tc.nc
 
-    def cast(engine, dst, src):
-        if engine == "g":
-            nc.gpsimd.tensor_scalar(out=dst, in0=src, scalar1=1.0, scalar2=0.0, op0=ALU.mult, op1=ALU.add)
-        elif engine == "s":
-            nc.scalar.copy(out=dst, in_=src)
-        else:
-            nc.vector.tensor_copy(out=dst, in_=src)
-
     with ExitStack() as ctx:
         keep = ctx.enter_context(tc.tile_pool(name="keep", bufs=1))
+        reuse = ctx.enter_context(tc.tile_pool(name="reuse", bufs=1))
         work = ctx.enter_context(tc.tile_pool(name="work", bufs=3))
         psum = ctx.enter_context(tc.psum_pool(name="psum", bufs=1))
 
@@ -58,10 +50,11 @@ def tile_list_factor_risk_allocation_kernel(
         nc.sync.dma_start(wsc_v[:], wv_scales.rearrange("a q y -> q a y").bitcast(I32))
         nc.sync.dma_start(wsc_r[:], wr_scales.rearrange("a q y -> q a y").bitcast(I32))
 
-        tab0 = keep.tile([P, T], I32, name="tab0", tag="first", align_bytes=64)
-        wv_raw = keep.tile([P, PASSES, H], I32, name="wv_raw", align_bytes=64)
+        tab0 = reuse.tile([P, T], I32, name="tab0", align_bytes=64, offset=0)
         nc.sync.dma_start(tab0[:], tab_words[0].rearrange("p t i -> p (t i)").bitcast(I32))
-        nc.sync.dma_start(wv_raw[:], wv_words.rearrange("a p y i -> p a (y i)").bitcast(I32))
+        wv_both = keep.tile([P, PASSES, H], I32, name="wv_both", align_bytes=64)
+        nc.sync.dma_start(wv_both[:], wv_words.rearrange("a p y i -> p a (y i)").bitcast(I32))
+        wv_raw = (wv_both[:, 0, :], wv_both[:, 1, :])
 
         PW = (S + 2 * H) // 4
         planes = keep.tile([P, PASSES, PW], I32, name="planes", align_bytes=64)
@@ -79,8 +72,7 @@ def tile_list_factor_risk_allocation_kernel(
             nc.sync.dma_start(planes[32 * q : 32 * q + 4, :, :], stage[8 * q : 8 * q + 8, :])
         tab1 = keep.tile([P, T], I32, name="tab1", tag="second", align_bytes=64)
         nc.sync.dma_start(tab1[:], tab_words[1].rearrange("p t i -> p (t i)").bitcast(I32))
-        wr_raw = keep.tile([P, PASSES, H // 2], I32, name="wr_raw", tag="third", align_bytes=64)
-        nc.sync.dma_start(wr_raw[:], wr_words.rearrange("a p y -> p a y").bitcast(I32))
+
         planes8 = planes[:].bitcast(U8)
 
         def v_scale(a, lo, n):
@@ -98,102 +90,126 @@ def tile_list_factor_risk_allocation_kernel(
             win = (tab0[:], tab1[:])[a]
             nc.vector.tensor_copy(vq[a][b][:], win.bitcast(U32).indirect(offsets[:, 32 * b : 32 * (b + 1)]))
 
-        wv_q = keep.tile([P, PASSES, H], I32, name="wv_q", align_bytes=64)
+        wv_q = [keep.tile([P, H], I32, name="wv_q%d" % a, align_bytes=64) for a in range(PASSES)]
         wr_q = keep.tile([P, PASSES, H // 2], I32, name="wr_q", align_bytes=64)
 
-        def permute(dst, src, run):
-            for a in range(PASSES):
-                nc.vector.tensor_copy(
-                    out=dst[:, a, :].rearrange("p (t g i) -> p t g i", t=4, i=run),
-                    in_=src[:, a, :].rearrange("p (g t i) -> p t g i", t=4, i=run),
-                )
-
-        def c_pass(acc, a, b, t):
-            nc.tensor.matmul_mx(
-                out=acc[:], lhsT=wv_q[:, a, P * t : P * (t + 1)].bitcast(FP8X4), lhsT_scale=wv_scale(a, t),
-                rhs=vq[a][b][:].bitcast(FP8X4), rhs_scale=v_scale(a, HALF * b, HALF), start=(a == 0), stop=(a == 1),
+        def permute_wv(a):
+            nc.vector.tensor_copy(
+                out=wv_q[a][:].rearrange("p (t g i) -> p t g i", t=4, i=4),
+                in_=wv_raw[a].rearrange("p (g t i) -> p t g i", t=4, i=4),
             )
 
-        def m_pass(acc, a, b, t):
+        c_acc = [[psum.tile([P, HALF], F32, name="c%d%d" % (b, t), tag="bank%d" % (4 * b + t)) for t in range(4)] for b in range(2)]
+
+        def c_pass(a, b, t):
             nc.tensor.matmul_mx(
-                out=acc[:], lhsT=wr_q[:, a, 64 * t : 64 * (t + 1)].bitcast(U8).bitcast(FP4X4), lhsT_scale=wr_scale(a, t),
+                out=c_acc[b][t][:], lhsT=wv_q[a][:, P * t : P * (t + 1)].bitcast(FP8X4), lhsT_scale=wv_scale(a, t),
                 rhs=vq[a][b][:].bitcast(FP8X4), rhs_scale=v_scale(a, HALF * b, HALF), start=(a == 0), stop=(a == 1),
             )
 
         gather(0, 0)
         gather(0, 1)
-        permute(wv_q, wv_raw, 4)
+        permute_wv(0)
+        permute_wv(1)
 
-        late = keep.tile([P, 5 * 1024], F32, name="late", tag="first", align_bytes=64)
-        we_raw = late[:, 0:4096].rearrange("p (a j r) -> p a j r", a=2, j=4)
-        wa_raw = late[:, 4096:5120].rearrange("p (t n) -> p t n", t=4)
-        for a in range(PASSES):
-            nc.sync.dma_start(we_raw[:, a], we[512 * a : 512 * (a + 1), :].rearrange("(p j) r -> p j r", j=4))
-        wa_rows = wa.rearrange("(g t i) n -> t g i n", t=4, i=4)
-        for t in range(4):
-            nc.sync.dma_start(wa_raw[:, t, :], wa_rows[t])
-
-        c_acc = [[psum.tile([P, HALF], F32, name="c%d%d" % (b, t), tag="bank%d" % (4 * b + t)) for t in range(4)] for b in range(2)]
-        for b in range(2):
-            for t in range(4):
-                c_pass(c_acc[b][t], 0, b, t)
-        gather(1, 0)
-        gather(1, 1)
-        nc.vector.tensor_copy(
-            out=wr_q[:].rearrange("p a (t g i) -> p a t g i", t=4, i=2),
-            in_=wr_raw[:].rearrange("p a (g t i) -> p a t g i", t=4, i=2),
-        )
-        for b in range(2):
-            for t in range(4):
-                c_pass(c_acc[b][t], 1, b, t)
+        wr_raw = reuse.tile([P, PASSES, H // 2], I32, name="wr_raw", align_bytes=64, offset=0)
+        slots = reuse.tile([P, 8 * HALF], F32, name="slots", align_bytes=64, offset=6 * KIB)
+        we0_raw, we1_raw = [slots[:, lo * HALF : (lo + 4) * HALF].rearrange("p (j r) -> p j r", j=4) for lo in (0, 4)]
+        we_raw = (we0_raw, we1_raw)
+        wa_raw = slots[:, HALF : 3 * HALF].rearrange("p (t n) -> p t n", t=4)
+        nc.sync.dma_start(wr_raw[:], wr_words.rearrange("a p y -> p a y").bitcast(I32))
+        nc.sync.dma_start(we0_raw, we[0:512, :].rearrange("(p j) r -> p j r", j=4))
+        nc.sync.dma_start(we1_raw, we[512:1024, :].rearrange("(p j) r -> p j r", j=4))
 
         damp = [keep.tile([P, 4, HALF], F32, name="damp%d" % b, align_bytes=64) for b in range(2)]
-        md = [keep.tile([P, 4, HALF], F32, name="md%d" % b, align_bytes=64) for b in range(2)]
-        we_bf = [keep.tile([P, 4, P, 4], BF16, name="we_bf%d" % a, align_bytes=64) for a in range(PASSES)]
-        we_q = keep.tile([P, PASSES, H], U32, name="we_q", align_bytes=64)
-        we_s = keep.tile([P, PASSES, H], U8, name="we_s", align_bytes=64)
-        wa_bf = keep.tile([P, N, 4], BF16, name="wa_bf", align_bytes=64)
+        md = [slots[:, lo * HALF : (lo + 4) * HALF].rearrange("p (t n) -> p t n", t=4) for lo in (3, 1)]
+        we_bf = [keep.tile([P, 4, P, 4], BF16, name="we_bf%d" % a, tag="we_bf%d" % a, align_bytes=64) for a in range(PASSES)]
+        we_q = [keep.tile([P, H], U32, name="we_q%d" % a, align_bytes=64) for a in range(PASSES)]
+        we_s = [keep.tile([P, H], U8, name="we_s%d" % a, align_bytes=64) for a in range(PASSES)]
         wa_q = keep.tile([P, N], U32, name="wa_q", align_bytes=64)
         wa_s = keep.tile([P, N], U8, name="wa_s", align_bytes=64)
-
-        def damping(b, t):
-            sq = work.tile([P, HALF], F32, name="sq", align_bytes=64)
-            nc.scalar.activation(out=sq[:], in_=c_acc[b][t][:], func=ACT.Square)
-            nc.scalar.activation(out=damp[b][:, t, :], in_=sq[:], func=ACT.Abs_reciprocal_sqrt, bias=1.0)
-
-        def forecast(b, t, bank):
-            acc = psum.tile([P, HALF], F32, name="m", tag="bank%d" % bank)
-            for a in range(PASSES):
-                m_pass(acc, a, b, t)
-            nc.vector.tensor_tensor(out=md[b][:, t, :], in0=acc[:], in1=damp[b][:, t, :], op=ALU.mult)
-
-        def cast_we(a):
-            for t in range(4):
-                dst = we_bf[a][:, t].rearrange("p (g u e) j -> p g u j e", u=2, e=2)
-                src = we_raw[:, a].rearrange("p j (g t u e) -> p t g u j e", t=4, u=2, e=2)[:, t]
-                cast(CAST_ENGINES[a][t], dst, src)
-
-        def quant_we(a):
-            nc.vector.quantize_mx(
-                out=we_q[:, a, :].bitcast(FP8X4), scales=we_s[:, a, :],
-                in_=we_bf[a][:].rearrange("p t c j -> p (t c j)"),
-            )
-
         h_bf = keep.tile([P, S, 4], BF16, name="h_bf", align_bytes=64)
         h_q = keep.tile([P, S], U32, name="h_q", align_bytes=64)
         h_s = keep.tile([P, S], U8, name="h_s", align_bytes=64)
         out_v = out.rearrange("(u p) j -> p u j", p=P)
 
+        wa_bf = keep.tile([P, N, 4], BF16, name="wa_bf", tag="we_bf1", align_bytes=64)
+
+        def load_wa():
+            wa_rows = wa.rearrange("(g t i) n -> t g i n", t=4, i=4)
+            for t in range(4):
+                nc.sync.dma_start(wa_raw[:, t, :], wa_rows[t])
+
+        def permute_wr():
+            nc.vector.tensor_copy(
+                out=wr_q[:].rearrange("p a (t g i) -> p a t g i", t=4, i=2),
+                in_=wr_raw[:].rearrange("p a (g t i) -> p a t g i", t=4, i=2),
+            )
+
+        sq = [keep.tile([P, 4, HALF], F32, name="sq%d" % b, align_bytes=64) for b in range(2)]
+
+        def square(b, t):
+            nc.scalar.activation(out=sq[b][:, t, :], in_=c_acc[b][t][:], func=ACT.Square)
+
+        def root(b, t, cols=slice(0, HALF)):
+            nc.scalar.activation(out=damp[b][:, t, cols], in_=sq[b][:, t, cols], func=ACT.Abs_reciprocal_sqrt, bias=1.0)
+
+        def m_sum(b, t, bank):
+            acc = psum.tile([P, HALF], F32, name="m", tag="bank%d" % bank)
+            for a in range(PASSES):
+                nc.tensor.matmul_mx(
+                    out=acc[:], lhsT=wr_q[:, a, 64 * t : 64 * (t + 1)].bitcast(U8).bitcast(FP4X4), lhsT_scale=wr_scale(a, t),
+                    rhs=vq[a][b][:].bitcast(FP8X4), rhs_scale=v_scale(a, HALF * b, HALF), start=(a == 0), stop=(a == 1),
+                )
+            return acc
+
+        def forecast(b, t, bank, parts=1):
+            acc = m_sum(b, t, bank)
+            for i in range(parts):
+                cols = slice(HALF // parts * i, HALF // parts * (i + 1))
+                nc.vector.tensor_tensor(out=md[b][:, t, cols], in0=acc[:, cols], in1=damp[b][:, t, cols], op=ALU.mult)
+
+        def forecast_aside(b, t, bank):
+            acc = m_sum(b, t, bank)
+            m_sb = work.tile([P, HALF], F32, name="m_sb", align_bytes=64)
+            nc.scalar.copy(out=m_sb[:], in_=acc[:])
+            nc.gpsimd.tensor_tensor(out=md[b][:, t, :], in0=m_sb[:], in1=damp[b][:, t, :], op=ALU.mult)
+
+        def we_views(a, slots):
+            dst = we_bf[a][:, slots].rearrange("p t (g i) j -> p t g j i", i=4)
+            src = we_raw[a].rearrange("p j (g t i) -> p t g j i", t=4, i=4)[:, slots]
+            return dst, src
+
+        def round_we_vector(a, lo, hi):
+            dst, src = we_views(a, slice(lo, hi))
+            nc.vector.tensor_copy(out=dst, in_=src)
+
+        def quant_we(a, lo=0, hi=4):
+            cols = slice(P * lo, P * hi)
+            nc.vector.quantize_mx(
+                out=we_q[a][:, cols].bitcast(FP8X4), scales=we_s[a][:, cols],
+                in_=we_bf[a][:, lo:hi].rearrange("p t c j -> p (t c j)"),
+            )
+
+        def round_wa_gpsimd(u):
+            nc.gpsimd.tensor_scalar(
+                out=wa_bf[:, P * u : P * (u + 1), :], in0=wa_raw[:, :, P * u : P * (u + 1)].rearrange("p t n -> p n t"),
+                scalar1=1.0, scalar2=0.0, op0=ALU.mult, op1=ALU.add,
+            )
+
+        def quant_wa():
+            nc.vector.quantize_mx(out=wa_q[:].bitcast(FP8X4), scales=wa_s[:], in_=wa_bf[:].rearrange("p n t -> p (n t)"))
+
         def exposure(s, bank):
             b, lo = divmod(TOK * s, HALF)
             acc = psum.tile([P, 4, TOK], F32, name="e", tag="bank%d" % bank)
             for t in range(4):
-                for a in range(PASSES):
+                for a in (1, 0):
                     nc.tensor.matmul_mx(
-                        out=acc[:, t, :], lhsT=we_q[:, a, P * t : P * (t + 1)].bitcast(FP8X4),
-                        lhsT_scale=we_s[:, a, P * t : P * (t + 1)],
+                        out=acc[:, t, :], lhsT=we_q[a][:, P * t : P * (t + 1)].bitcast(FP8X4),
+                        lhsT_scale=we_s[a][:, P * t : P * (t + 1)],
                         rhs=vq[a][b][:, lo : lo + TOK].bitcast(FP8X4), rhs_scale=v_scale(a, TOK * s, TOK),
-                        start=(a == 0), stop=(a == 1),
+                        start=(a == 1), stop=(a == 0),
                     )
             nc.vector.tensor_tensor(
                 out=h_bf[:, TOK * s : TOK * (s + 1), :].rearrange("p (c i) t -> p c t i", i=4),
@@ -202,9 +218,9 @@ def tile_list_factor_risk_allocation_kernel(
                 op=ALU.mult,
             )
 
-        def allocate(group, bank):
-            lo, width = TOK * group[0], TOK * len(group)
-            cols = slice(lo, lo + width)
+        def allocate(first, count, bank):
+            cols = slice(TOK * first, TOK * (first + count))
+            width = TOK * count
             nc.vector.quantize_mx(
                 out=h_q[:, cols].bitcast(FP8X4), scales=h_s[:, cols],
                 in_=h_bf[:, cols, :].rearrange("p n t -> p (n t)"),
@@ -220,29 +236,57 @@ def tile_list_factor_risk_allocation_kernel(
             nc.scalar.copy(out=res[:], in_=acc[:])
             nc.sync.dma_start(out_v[:, :, cols], res[:])
 
-        damping(0, 0)
-        damping(0, 1)
-        cast_we(0)
+        for b in range(2):
+            for t in range(4):
+                c_pass(0, b, t)
+        gather(1, 0)
+        gather(1, 1)
+        for t in range(4):
+            c_pass(1, 0, t)
+        for pair in ((0, 1), (2, 3)):
+            for t in pair:
+                square(0, t)
+            for t in pair:
+                root(0, t)
+        permute_wr()
+        round_we_vector(0, 0, 2)
+        round_we_vector(0, 2, 4)
+        load_wa()
         forecast(0, 0, 0)
         quant_we(0)
+        round_we_vector(1, 0, 4)
         forecast(0, 1, 1)
-        cast_we(1)
         quant_we(1)
-        for t in (2, 3):
-            damping(0, t)
-            forecast(0, t, t)
         for t in range(4):
-            damping(1, t)
-            exposure(t, t)
-            forecast(1, t, 4 + t)
-        cast(WA_ENGINE, wa_bf[:].rearrange("p (c i) t -> p c t i", i=2), wa_raw.rearrange("p t (c i) -> p c t i", i=2))
-        nc.vector.quantize_mx(out=wa_q[:].bitcast(FP8X4), scales=wa_s[:], in_=wa_bf[:].rearrange("p n t -> p (n t)"))
+            c_pass(1, 1, t)
+        forecast(0, 2, 2)
+        forecast(0, 3, 3)
+        round_wa_gpsimd(0)
+        round_wa_gpsimd(1)
+        square(1, 0)
+        square(1, 1)
+        root(1, 0)
+        exposure(0, 4)
+        forecast_aside(1, 0, 0)
+        root(1, 1)
+        exposure(1, 5)
+        forecast_aside(1, 1, 1)
+        square(1, 2)
+        square(1, 3)
+        root(1, 2)
+        root(1, 3, slice(0, 256))
+        root(1, 3, slice(256, 512))
+        exposure(2, 2)
+        exposure(3, 3)
+        forecast(1, 2, 4)
+        forecast(1, 3, 5, 2)
+        quant_wa()
+        allocate(0, 2, 5)
         exposure(4, 0)
-        allocate([0, 1], 4)
-        exposure(5, 1)
-        allocate([2, 3], 5)
-        exposure(6, 2)
-        allocate([4, 5], 6)
-        exposure(7, 3)
-        allocate([6], 7)
-        allocate([7], 4)
+        allocate(2, 2, 1)
+        exposure(5, 6)
+        exposure(6, 7)
+        allocate(4, 2, 2)
+        exposure(7, 0)
+        allocate(6, 1, 3)
+        allocate(7, 1, 4)

@@ -84,7 +84,7 @@ def tile_list_factor_risk_allocation_kernel(
         def wr_scale(a, t):
             return planes8[:, a, S + H + P * t : S + H + P * (t + 1)]
 
-        vq = [[keep.tile([P, HALF], U32, name="vq%d%d" % (a, b), align_bytes=64) for b in range(2)] for a in range(PASSES)]
+        vq = [[keep.tile([P, HALF], U32, name="vq%d%d" % (a, b), tag="vq%d%d" % (a, b), align_bytes=64) for b in range(2)] for a in range(PASSES)]
 
         def gather(a, b):
             win = (tab0[:], tab1[:])[a]
@@ -126,10 +126,10 @@ def tile_list_factor_risk_allocation_kernel(
         we_bf = [keep.tile([P, 4, P, 4], BF16, name="we_bf%d" % a, tag="we_bf%d" % a, align_bytes=64) for a in range(PASSES)]
         we_q = [keep.tile([P, H], U32, name="we_q%d" % a, align_bytes=64) for a in range(PASSES)]
         we_s = [keep.tile([P, H], U8, name="we_s%d" % a, align_bytes=64) for a in range(PASSES)]
-        wa_q = keep.tile([P, N], U32, name="wa_q", align_bytes=64)
+        wa_q = keep.tile([P, N], U32, name="wa_q", tag="vq00", align_bytes=64)
         wa_s = keep.tile([P, N], U8, name="wa_s", align_bytes=64)
         h_bf = keep.tile([P, S, 4], BF16, name="h_bf", align_bytes=64)
-        h_q = keep.tile([P, S], U32, name="h_q", align_bytes=64)
+        h_q = keep.tile([P, S], U32, name="h_q", tag="vq10", align_bytes=64)
         h_s = keep.tile([P, S], U8, name="h_s", align_bytes=64)
         out_v = out.rearrange("(u p) j -> p u j", p=P)
 
@@ -169,10 +169,13 @@ def tile_list_factor_risk_allocation_kernel(
                 cols = slice(HALF // parts * i, HALF // parts * (i + 1))
                 nc.vector.tensor_tensor(out=md[b][:, t, cols], in0=acc[:, cols], in1=damp[b][:, t, cols], op=ALU.mult)
 
-        def forecast_aside(b, t, bank):
+        def copy_m(b, t, bank):
             acc = m_sum(b, t, bank)
             m_sb = work.tile([P, HALF], F32, name="m_sb", align_bytes=64)
             nc.scalar.copy(out=m_sb[:], in_=acc[:])
+            return m_sb
+
+        def forecast_gpsimd(b, t, m_sb):
             nc.gpsimd.tensor_tensor(out=md[b][:, t, :], in0=m_sb[:], in1=damp[b][:, t, :], op=ALU.mult)
 
         def we_views(a, slots):
@@ -218,13 +221,16 @@ def tile_list_factor_risk_allocation_kernel(
                 op=ALU.mult,
             )
 
-        def allocate(first, count, bank):
+        def quant_h(first, count):
             cols = slice(TOK * first, TOK * (first + count))
-            width = TOK * count
             nc.vector.quantize_mx(
                 out=h_q[:, cols].bitcast(FP8X4), scales=h_s[:, cols],
                 in_=h_bf[:, cols, :].rearrange("p n t -> p (n t)"),
             )
+
+        def allocate(first, count, bank, copy=nc.scalar.copy):
+            cols = slice(TOK * first, TOK * (first + count))
+            width = TOK * count
             acc = psum.tile([P, 2, width], F32, name="o", tag="bank%d" % bank)
             for u in range(2):
                 nc.tensor.matmul_mx(
@@ -232,8 +238,8 @@ def tile_list_factor_risk_allocation_kernel(
                     lhsT_scale=wa_s[:, P * u : P * (u + 1)],
                     rhs=h_q[:, cols].bitcast(FP8X4), rhs_scale=h_s[:, cols], start=True, stop=True,
                 )
-            res = work.tile([P, 2, width], F32, name="res", tag="res", bufs=5, align_bytes=64)
-            nc.scalar.copy(out=res[:], in_=acc[:])
+            res = work.tile([P, 2, width], F32, name="res", tag="res", bufs=6, align_bytes=64)
+            copy(out=res[:], in_=acc[:])
             nc.sync.dma_start(out_v[:, :, cols], res[:])
 
         for b in range(2):
@@ -252,11 +258,14 @@ def tile_list_factor_risk_allocation_kernel(
         round_we_vector(0, 0, 2)
         round_we_vector(0, 2, 4)
         load_wa()
+        quant_we(0, 0, 2)
         forecast(0, 0, 0)
-        quant_we(0)
-        round_we_vector(1, 0, 4)
+        quant_we(0, 2, 4)
+        round_we_vector(1, 2, 4)
+        round_we_vector(1, 0, 2)
+        quant_we(1, 2, 4)
         forecast(0, 1, 1)
-        quant_we(1)
+        quant_we(1, 0, 2)
         for t in range(4):
             c_pass(1, 1, t)
         forecast(0, 2, 2)
@@ -266,11 +275,11 @@ def tile_list_factor_risk_allocation_kernel(
         square(1, 0)
         square(1, 1)
         root(1, 0)
-        exposure(0, 4)
-        forecast_aside(1, 0, 0)
+        exposure(0, 1)
+        forecast_gpsimd(1, 0, copy_m(1, 0, 0))
         root(1, 1)
         exposure(1, 5)
-        forecast_aside(1, 1, 1)
+        forecast_gpsimd(1, 1, copy_m(1, 1, 4))
         square(1, 2)
         square(1, 3)
         root(1, 2)
@@ -278,15 +287,22 @@ def tile_list_factor_risk_allocation_kernel(
         root(1, 3, slice(256, 512))
         exposure(2, 2)
         exposure(3, 3)
-        forecast(1, 2, 4)
-        forecast(1, 3, 5, 2)
         quant_wa()
+        quant_h(0, 2)
+        quant_h(2, 2)
+        forecast(1, 2, 1)
+        forecast(1, 3, 5, 2)
         allocate(0, 2, 5)
         exposure(4, 0)
-        allocate(2, 2, 1)
+        allocate(2, 2, 4)
         exposure(5, 6)
+        quant_h(4, 1)
+        allocate(4, 1, 2)
         exposure(6, 7)
-        allocate(4, 2, 2)
+        quant_h(5, 1)
+        allocate(5, 1, 3)
         exposure(7, 0)
-        allocate(6, 1, 3)
-        allocate(7, 1, 4)
+        quant_h(6, 1)
+        allocate(6, 1, 1)
+        quant_h(7, 1)
+        allocate(7, 1, 6, nc.vector.tensor_copy)

@@ -50,7 +50,7 @@ def tile_list_factor_risk_allocation_kernel(
         nc.sync.dma_start(wsc_v[:], wv_scales.rearrange("a q y -> q a y").bitcast(I32))
         nc.sync.dma_start(wsc_r[:], wr_scales.rearrange("a q y -> q a y").bitcast(I32))
 
-        tab0 = reuse.tile([P, T], I32, name="tab0", align_bytes=64, offset=0)
+        tab0 = reuse.tile([P, T], I32, name="tab0", align_bytes=64, offset=8 * KIB)
         nc.sync.dma_start(tab0[:], tab_words[0].rearrange("p t i -> p (t i)").bitcast(I32))
         wv_both = keep.tile([P, PASSES, H], I32, name="wv_both", align_bytes=64)
         nc.sync.dma_start(wv_both[:], wv_words.rearrange("a p y i -> p a (y i)").bitcast(I32))
@@ -112,17 +112,18 @@ def tile_list_factor_risk_allocation_kernel(
         permute_wv(0)
         permute_wv(1)
 
-        wr_raw = reuse.tile([P, PASSES, H // 2], I32, name="wr_raw", align_bytes=64, offset=0)
-        slots = reuse.tile([P, 8 * HALF], F32, name="slots", align_bytes=64, offset=6 * KIB)
+        wr_raw = reuse.tile([P, PASSES, H // 2], I32, name="wr_raw", align_bytes=64, offset=20 * KIB)
+        slots = reuse.tile([P, 8 * HALF], F32, name="slots", align_bytes=64, offset=4 * KIB)
         we0_raw, we1_raw = [slots[:, lo * HALF : (lo + 4) * HALF].rearrange("p (j r) -> p j r", j=4) for lo in (0, 4)]
         we_raw = (we0_raw, we1_raw)
-        wa_raw = slots[:, HALF : 3 * HALF].rearrange("p (t n) -> p t n", t=4)
+        wa_raw = reuse.tile([P, 4, N], F32, name="wa_raw", align_bytes=64, offset=22 * KIB)
         nc.sync.dma_start(wr_raw[:], wr_words.rearrange("a p y -> p a y").bitcast(I32))
         nc.sync.dma_start(we0_raw, we[0:512, :].rearrange("(p j) r -> p j r", j=4))
         nc.sync.dma_start(we1_raw, we[512:1024, :].rearrange("(p j) r -> p j r", j=4))
 
         damp = [keep.tile([P, 4, HALF], F32, name="damp%d" % b, align_bytes=64) for b in range(2)]
-        md = [slots[:, lo * HALF : (lo + 4) * HALF].rearrange("p (t n) -> p t n", t=4) for lo in (3, 1)]
+        md1 = reuse.tile([P, 4, HALF], F32, name="md1", align_bytes=64, offset=22 * KIB)
+        md = [slots[:, 3 * HALF : 7 * HALF].rearrange("p (t n) -> p t n", t=4), md1[:]]
         we_bf = [keep.tile([P, 4, P, 4], BF16, name="we_bf%d" % a, tag="we_bf%d" % a, align_bytes=64) for a in range(PASSES)]
         we_q = [keep.tile([P, H], U32, name="we_q%d" % a, align_bytes=64) for a in range(PASSES)]
         we_s = [keep.tile([P, H], U8, name="we_s%d" % a, align_bytes=64) for a in range(PASSES)]
@@ -155,7 +156,7 @@ def tile_list_factor_risk_allocation_kernel(
             nc.scalar.activation(out=damp[b][:, t, cols], in_=sq[b][:, t, cols], func=ACT.Abs_reciprocal_sqrt, bias=1.0)
 
         def m_sum(b, t, bank):
-            acc = psum.tile([P, HALF], F32, name="m", tag="bank%d" % bank)
+            acc = psum.tile([P, HALF], F32, name="m%d%d" % (b, t), tag="bank%d" % bank)
             for a in range(PASSES):
                 nc.tensor.matmul_mx(
                     out=acc[:], lhsT=wr_q[:, a, 64 * t : 64 * (t + 1)].bitcast(U8).bitcast(FP4X4), lhsT_scale=wr_scale(a, t),
@@ -194,9 +195,9 @@ def tile_list_factor_risk_allocation_kernel(
                 in_=we_bf[a][:, lo:hi].rearrange("p t c j -> p (t c j)"),
             )
 
-        def round_wa_gpsimd(u):
+        def round_wa_gpsimd():
             nc.gpsimd.tensor_scalar(
-                out=wa_bf[:, P * u : P * (u + 1), :], in0=wa_raw[:, :, P * u : P * (u + 1)].rearrange("p t n -> p n t"),
+                out=wa_bf[:], in0=wa_raw[:].rearrange("p t n -> p n t"),
                 scalar1=1.0, scalar2=0.0, op0=ALU.mult, op1=ALU.add,
             )
 
@@ -205,8 +206,8 @@ def tile_list_factor_risk_allocation_kernel(
 
         def exposure(s, bank):
             b, lo = divmod(TOK * s, HALF)
-            acc = psum.tile([P, 4, TOK], F32, name="e", tag="bank%d" % bank)
-            for t in range(4):
+            acc = psum.tile([P, 4, TOK], F32, name="e%d" % s, tag="bank%d" % bank)
+            for t in (2, 3, 0, 1):
                 for a in (1, 0):
                     nc.tensor.matmul_mx(
                         out=acc[:, t, :], lhsT=we_q[a][:, P * t : P * (t + 1)].bitcast(FP8X4),
@@ -214,31 +215,38 @@ def tile_list_factor_risk_allocation_kernel(
                         rhs=vq[a][b][:, lo : lo + TOK].bitcast(FP8X4), rhs_scale=v_scale(a, TOK * s, TOK),
                         start=(a == 1), stop=(a == 0),
                     )
+            return acc
+
+        def contribute(s, acc, first=0, count=TOK):
+            b, lo = divmod(TOK * s + first, HALF)
             nc.vector.tensor_tensor(
-                out=h_bf[:, TOK * s : TOK * (s + 1), :].rearrange("p (c i) t -> p c t i", i=4),
-                in0=acc[:].rearrange("p t (c i) -> p c t i", i=4),
-                in1=md[b][:, :, lo : lo + TOK].rearrange("p t (c i) -> p c t i", i=4),
+                out=h_bf[:, HALF * b + lo : HALF * b + lo + count, :].rearrange("p (c i) t -> p c t i", i=4),
+                in0=acc[:, :, first : first + count].rearrange("p t (c i) -> p c t i", i=4),
+                in1=md[b][:, :, lo : lo + count].rearrange("p t (c i) -> p c t i", i=4),
                 op=ALU.mult,
             )
 
         def quant_h(first, count):
-            cols = slice(TOK * first, TOK * (first + count))
+            cols = slice(int(TOK * first), int(TOK * (first + count)))
             nc.vector.quantize_mx(
                 out=h_q[:, cols].bitcast(FP8X4), scales=h_s[:, cols],
                 in_=h_bf[:, cols, :].rearrange("p n t -> p (n t)"),
             )
 
-        def allocate(first, count, bank, copy=nc.scalar.copy):
-            cols = slice(TOK * first, TOK * (first + count))
-            width = TOK * count
-            acc = psum.tile([P, 2, width], F32, name="o", tag="bank%d" % bank)
+        def allocate(first, count, bank, copy=nc.scalar.copy, into=None):
+            cols = slice(int(TOK * first), int(TOK * (first + count)))
+            width = int(TOK * count)
+            acc = psum.tile([P, 2, width], F32, name="o%d" % first, tag="bank%d" % bank)
             for u in range(2):
                 nc.tensor.matmul_mx(
                     out=acc[:, u, :], lhsT=wa_q[:, P * u : P * (u + 1)].bitcast(FP8X4),
                     lhsT_scale=wa_s[:, P * u : P * (u + 1)],
                     rhs=h_q[:, cols].bitcast(FP8X4), rhs_scale=h_s[:, cols], start=True, stop=True,
                 )
-            res = work.tile([P, 2, width], F32, name="res", tag="res", bufs=6, align_bytes=64)
+            if into is not None:
+                copy(out=into, in_=acc[:])
+                return
+            res = work.tile([P, 2, width], F32, name="res", tag="res", bufs=7, align_bytes=64)
             copy(out=res[:], in_=acc[:])
             nc.sync.dma_start(out_v[:, :, cols], res[:])
 
@@ -249,11 +257,18 @@ def tile_list_factor_risk_allocation_kernel(
         gather(1, 1)
         for t in range(4):
             c_pass(1, 0, t)
-        for pair in ((0, 1), (2, 3)):
-            for t in pair:
-                square(0, t)
-            for t in pair:
-                root(0, t)
+        c_pass(1, 1, 0)
+        c_pass(1, 1, 1)
+        square(0, 0)
+        square(0, 1)
+        root(0, 0)
+        root(0, 1)
+        square(0, 2)
+        square(0, 3)
+        root(0, 2)
+        square(1, 0)
+        square(1, 1)
+        root(0, 3)
         permute_wr()
         round_we_vector(0, 0, 2)
         round_we_vector(0, 2, 4)
@@ -264,45 +279,51 @@ def tile_list_factor_risk_allocation_kernel(
         round_we_vector(1, 2, 4)
         round_we_vector(1, 0, 2)
         quant_we(1, 2, 4)
-        forecast(0, 1, 1)
         quant_we(1, 0, 2)
-        for t in range(4):
-            c_pass(1, 1, t)
+        forecast(0, 1, 1)
+        c_pass(1, 1, 2)
+        c_pass(1, 1, 3)
         forecast(0, 2, 2)
         forecast(0, 3, 3)
-        round_wa_gpsimd(0)
-        round_wa_gpsimd(1)
-        square(1, 0)
-        square(1, 1)
+        round_wa_gpsimd()
         root(1, 0)
-        exposure(0, 1)
         forecast_gpsimd(1, 0, copy_m(1, 0, 0))
         root(1, 1)
-        exposure(1, 5)
         forecast_gpsimd(1, 1, copy_m(1, 1, 4))
         square(1, 2)
         square(1, 3)
         root(1, 2)
         root(1, 3, slice(0, 256))
         root(1, 3, slice(256, 512))
-        exposure(2, 2)
-        exposure(3, 3)
+        contribute(0, exposure(0, 5))
+        contribute(1, exposure(1, 1))
+        contribute(2, exposure(2, 2))
+        contribute(3, exposure(3, 3))
         quant_wa()
         quant_h(0, 2)
         quant_h(2, 2)
-        forecast(1, 2, 1)
-        forecast(1, 3, 5, 2)
-        allocate(0, 2, 5)
-        exposure(4, 0)
-        allocate(2, 2, 4)
-        exposure(5, 6)
+        forecast(1, 2, 5)
+        forecast(1, 3, 1, 2)
+        e4 = exposure(4, 2)
+        allocate(0, 2, 6)
+        contribute(4, e4)
+        e5 = exposure(5, 3)
+        allocate(2, 2, 7)
+        contribute(5, e5)
         quant_h(4, 1)
-        allocate(4, 1, 2)
-        exposure(6, 7)
+        e6 = exposure(6, 5)
+        allocate(4, 1, 0)
+        contribute(6, e6)
         quant_h(5, 1)
-        allocate(5, 1, 3)
-        exposure(7, 0)
+        e7 = exposure(7, 1)
+        allocate(5, 1, 4)
+        contribute(7, e7, 0, TOK // 2)
         quant_h(6, 1)
-        allocate(6, 1, 1)
-        quant_h(7, 1)
-        allocate(7, 1, 6, nc.vector.tensor_copy)
+        allocate(6, 1, 2)
+        contribute(7, e7, TOK // 2, TOK // 2)
+        quant_h(7, 0.5)
+        last = keep.tile([P, 2, TOK], F32, name="last", align_bytes=64)
+        allocate(7, 0.5, 3, nc.scalar.copy, last[:, :, 0 : TOK // 2])
+        quant_h(7.5, 0.5)
+        allocate(7.5, 0.5, 6, nc.vector.tensor_copy, last[:, :, TOK // 2 : TOK])
+        nc.sync.dma_start(out_v[:, :, S - TOK : S], last[:])

@@ -44,11 +44,10 @@ def tile_list_factor_risk_allocation_kernel(
         tsc = keep.tile([P, T // 4], I32, name="tsc", align_bytes=64)
         nc.vector.memset(tsc[32:64, :], 0)
         nc.vector.memset(tsc[64:128, :], 0)
-        wsc_r = keep.tile([32, H // 4], I32, name="wsc_r", align_bytes=64)
+        wsc_r = keep.tile([P, PASSES, H // 4], I32, name="wsc_r", align_bytes=64)
         wsc_v = keep.tile([32, H // 4], I32, name="wsc_v", align_bytes=64)
         nc.sync.dma_start(tsc[0:32, :], tab_scales.rearrange("a q t -> q a t").bitcast(I32))
         nc.sync.dma_start(wsc_v[:], wv_scales.rearrange("a q y -> q a y").bitcast(I32))
-        nc.sync.dma_start(wsc_r[:], wr_scales.rearrange("a q y -> q a y").bitcast(I32))
 
         tab0 = reuse.tile([P, T], I32, name="tab0", align_bytes=64, offset=8 * KIB)
         nc.sync.dma_start(tab0[:], tab_words[0].rearrange("p t i -> p (t i)").bitcast(I32))
@@ -56,13 +55,21 @@ def tile_list_factor_risk_allocation_kernel(
         nc.sync.dma_start(wv_both[:], wv_words.rearrange("a p y i -> p a (y i)").bitcast(I32))
         wv_raw = (wv_both[:, 0, :], wv_both[:, 1, :])
 
-        PW = (S + 2 * H) // 4
+        PW = (S + H) // 4
         planes = keep.tile([P, PASSES, PW], I32, name="planes", align_bytes=64)
         nc.gpsimd.memset(planes[:], 0)
+        nc.gpsimd.memset(wsc_r[:], 0)
+        for q in (0, 2, 1, 3):
+            rows = wr_scales[:, 4 * q : 4 * q + 4, :].rearrange("a r y -> r a y").bitcast(I32)
+            nc.gpsimd.dma_start(wsc_r[32 * q : 32 * q + 4], rows)
+        wr_s = keep.tile([P, PASSES, H // 4], I32, name="wr_s", align_bytes=64)
+        nc.gpsimd.tensor_copy(
+            out=wr_s[:].rearrange("p a (t g) -> p a t g", t=4), in_=wsc_r[:].rearrange("p a (g t) -> p a t g", t=4)
+        )
         sg = keep.tile([P, S], U8, name="sg", tag="second", align_bytes=64)
         nc.vector.tensor_copy(sg[:], tsc[:].bitcast(U8).indirect(offsets[:]))
         stage = keep.tile([32, PW], I32, name="stage", tag="third", align_bytes=64)
-        for src, lo in ((wsc_v, S // 4), (wsc_r, (S + H) // 4)):
+        for src, lo in ((wsc_v, S // 4),):
             nc.vector.tensor_copy(
                 out=stage[:, lo : lo + H // 4].rearrange("p (t c k) -> p c t k", t=4, k=4),
                 in_=src[:].rearrange("p (c k t) -> p c t k", t=4, k=4),
@@ -82,7 +89,7 @@ def tile_list_factor_risk_allocation_kernel(
             return planes8[:, a, S + P * t : S + P * (t + 1)]
 
         def wr_scale(a, t):
-            return planes8[:, a, S + H + P * t : S + H + P * (t + 1)]
+            return wr_s[:].bitcast(U8)[:, a, P * t : P * (t + 1)]
 
         vq = [[keep.tile([P, HALF], U32, name="vq%d%d" % (a, b), tag="vq%d%d" % (a, b), align_bytes=64) for b in range(2)] for a in range(PASSES)]
 
@@ -123,7 +130,7 @@ def tile_list_factor_risk_allocation_kernel(
 
         damp = [keep.tile([P, 4, HALF], F32, name="damp%d" % b, align_bytes=64) for b in range(2)]
         md1 = reuse.tile([P, 4, HALF], F32, name="md1", align_bytes=64, offset=22 * KIB)
-        md = [slots[:, 3 * HALF : 7 * HALF].rearrange("p (t n) -> p t n", t=4), md1[:]]
+        md = [slots[:, 2 * HALF : 6 * HALF].rearrange("p (t n) -> p t n", t=4), md1[:]]
         we_bf = [keep.tile([P, 4, P, 4], BF16, name="we_bf%d" % a, tag="we_bf%d" % a, align_bytes=64) for a in range(PASSES)]
         we_q = [keep.tile([P, H], U32, name="we_q%d" % a, align_bytes=64) for a in range(PASSES)]
         we_s = [keep.tile([P, H], U8, name="we_s%d" % a, align_bytes=64) for a in range(PASSES)]
@@ -276,15 +283,15 @@ def tile_list_factor_risk_allocation_kernel(
         quant_we(0, 0, 2)
         forecast(0, 0, 0)
         quant_we(0, 2, 4)
+        forecast(0, 1, 1)
         round_we_vector(1, 2, 4)
         round_we_vector(1, 0, 2)
         quant_we(1, 2, 4)
         quant_we(1, 0, 2)
-        forecast(0, 1, 1)
         c_pass(1, 1, 2)
         c_pass(1, 1, 3)
         forecast(0, 2, 2)
-        forecast(0, 3, 3)
+        forecast(0, 3, 3, 2)
         round_wa_gpsimd()
         root(1, 0)
         forecast_gpsimd(1, 0, copy_m(1, 0, 0))
@@ -295,15 +302,15 @@ def tile_list_factor_risk_allocation_kernel(
         root(1, 2)
         root(1, 3, slice(0, 256))
         root(1, 3, slice(256, 512))
-        contribute(0, exposure(0, 5))
-        contribute(1, exposure(1, 1))
+        contribute(0, exposure(0, 1))
+        contribute(1, exposure(1, 5))
         contribute(2, exposure(2, 2))
         contribute(3, exposure(3, 3))
         quant_wa()
         quant_h(0, 2)
         quant_h(2, 2)
-        forecast(1, 2, 5)
-        forecast(1, 3, 1, 2)
+        forecast(1, 2, 1)
+        forecast(1, 3, 5, 2)
         e4 = exposure(4, 2)
         allocate(0, 2, 6)
         contribute(4, e4)
@@ -311,11 +318,11 @@ def tile_list_factor_risk_allocation_kernel(
         allocate(2, 2, 7)
         contribute(5, e5)
         quant_h(4, 1)
-        e6 = exposure(6, 5)
+        e6 = exposure(6, 1)
         allocate(4, 1, 0)
         contribute(6, e6)
         quant_h(5, 1)
-        e7 = exposure(7, 1)
+        e7 = exposure(7, 5)
         allocate(5, 1, 4)
         contribute(7, e7, 0, TOK // 2)
         quant_h(6, 1)

@@ -41,34 +41,34 @@ def tile_list_factor_risk_allocation_kernel(
         nc.vector.memset(warm[:, 0:1], 1.0)
         nc.scalar.activation(out=warm[:, 1:2], in_=warm[:, 0:1], func=ACT.Abs_reciprocal_sqrt)
 
-        tsc = keep.tile([P, T // 4], I32, name="tsc", align_bytes=64)
+        tsc = keep.tile([P, T // 4], I32, name="tsc", align_bytes=256)
         nc.vector.memset(tsc[32:64, :], 0)
         nc.vector.memset(tsc[64:128, :], 0)
-        wsc_r = keep.tile([P, PASSES, H // 4], I32, name="wsc_r", align_bytes=64)
-        wsc_v = keep.tile([32, H // 4], I32, name="wsc_v", align_bytes=64)
+        wsc_r = keep.tile([P, PASSES, H // 4], I32, name="wsc_r", align_bytes=256)
+        wsc_v = keep.tile([32, H // 4], I32, name="wsc_v", align_bytes=256)
         nc.sync.dma_start(tsc[0:32, :], tab_scales.rearrange("a q t -> q a t").bitcast(I32))
         nc.sync.dma_start(wsc_v[:], wv_scales.rearrange("a q y -> q a y").bitcast(I32))
 
-        tab0 = reuse.tile([P, T], I32, name="tab0", align_bytes=64, offset=8 * KIB)
+        tab0 = reuse.tile([P, T], I32, name="tab0", align_bytes=256, offset=8 * KIB)
         nc.sync.dma_start(tab0[:], tab_words[0].rearrange("p t i -> p (t i)").bitcast(I32))
-        wv_both = keep.tile([P, PASSES, H], I32, name="wv_both", align_bytes=64)
+        wv_both = keep.tile([P, PASSES, H], I32, name="wv_both", align_bytes=256)
         nc.sync.dma_start(wv_both[:], wv_words.rearrange("a p y i -> p a (y i)").bitcast(I32))
         wv_raw = (wv_both[:, 0, :], wv_both[:, 1, :])
 
         PW = (S + H) // 4
-        planes = keep.tile([P, PASSES, PW], I32, name="planes", align_bytes=64)
+        planes = keep.tile([P, PASSES, PW], I32, name="planes", align_bytes=256)
         nc.gpsimd.memset(planes[:], 0)
         nc.gpsimd.memset(wsc_r[:], 0)
         for q in (0, 2, 1, 3):
             rows = wr_scales[:, 4 * q : 4 * q + 4, :].rearrange("a r y -> r a y").bitcast(I32)
             nc.gpsimd.dma_start(wsc_r[32 * q : 32 * q + 4], rows)
-        wr_s = keep.tile([P, PASSES, H // 4], I32, name="wr_s", align_bytes=64)
+        wr_s = keep.tile([P, PASSES, H // 4], I32, name="wr_s", align_bytes=256)
         nc.gpsimd.tensor_copy(
             out=wr_s[:].rearrange("p a (t g) -> p a t g", t=4), in_=wsc_r[:].rearrange("p a (g t) -> p a t g", t=4)
         )
-        sg = keep.tile([P, S], U8, name="sg", tag="second", align_bytes=64)
+        sg = keep.tile([P, S], U8, name="sg", tag="second", align_bytes=256)
         nc.vector.tensor_copy(sg[:], tsc[:].bitcast(U8).indirect(offsets[:]))
-        stage = keep.tile([32, PW], I32, name="stage", tag="third", align_bytes=64)
+        stage = keep.tile([32, PW], I32, name="stage", tag="third", align_bytes=256)
         for src, lo in ((wsc_v, S // 4),):
             nc.vector.tensor_copy(
                 out=stage[:, lo : lo + H // 4].rearrange("p (t c k) -> p c t k", t=4, k=4),
@@ -77,7 +77,7 @@ def tile_list_factor_risk_allocation_kernel(
         nc.vector.tensor_copy(out=stage[:, 0 : S // 4], in_=sg[0:32, :].bitcast(I32))
         for q in (0, 2, 1, 3):
             nc.sync.dma_start(planes[32 * q : 32 * q + 4, :, :], stage[8 * q : 8 * q + 8, :])
-        tab1 = keep.tile([P, T], I32, name="tab1", tag="second", align_bytes=64)
+        tab1 = keep.tile([P, T], I32, name="tab1", tag="second", align_bytes=256)
         nc.sync.dma_start(tab1[:], tab_words[1].rearrange("p t i -> p (t i)").bitcast(I32))
 
         planes8 = planes[:].bitcast(U8)
@@ -91,14 +91,14 @@ def tile_list_factor_risk_allocation_kernel(
         def wr_scale(a, t):
             return wr_s[:].bitcast(U8)[:, a, P * t : P * (t + 1)]
 
-        vq = [[keep.tile([P, HALF], U32, name="vq%d%d" % (a, b), tag="vq%d%d" % (a, b), align_bytes=64) for b in range(2)] for a in range(PASSES)]
+        vq = [[keep.tile([P, HALF], U32, name="vq%d%d" % (a, b), tag="vq%d%d" % (a, b), align_bytes=256) for b in range(2)] for a in range(PASSES)]
 
         def gather(a, b):
             win = (tab0[:], tab1[:])[a]
             nc.vector.tensor_copy(vq[a][b][:], win.bitcast(U32).indirect(offsets[:, 32 * b : 32 * (b + 1)]))
 
-        wv_q = [keep.tile([P, H], I32, name="wv_q%d" % a, align_bytes=64) for a in range(PASSES)]
-        wr_q = keep.tile([P, PASSES, H // 2], I32, name="wr_q", align_bytes=64)
+        wv_q = [keep.tile([P, H], I32, name="wv_q%d" % a, align_bytes=256) for a in range(PASSES)]
+        wr_q = keep.tile([P, PASSES, H // 2], I32, name="wr_q", align_bytes=256)
 
         def permute_wv(a):
             nc.vector.tensor_copy(
@@ -119,29 +119,29 @@ def tile_list_factor_risk_allocation_kernel(
         permute_wv(0)
         permute_wv(1)
 
-        wr_raw = reuse.tile([P, PASSES, H // 2], I32, name="wr_raw", align_bytes=64, offset=20 * KIB)
-        slots = reuse.tile([P, 8 * HALF], F32, name="slots", align_bytes=64, offset=4 * KIB)
+        wr_raw = reuse.tile([P, PASSES, H // 2], I32, name="wr_raw", align_bytes=256, offset=20 * KIB)
+        slots = reuse.tile([P, 8 * HALF], F32, name="slots", align_bytes=256, offset=4 * KIB)
         we0_raw, we1_raw = [slots[:, lo * HALF : (lo + 4) * HALF].rearrange("p (j r) -> p j r", j=4) for lo in (0, 4)]
         we_raw = (we0_raw, we1_raw)
-        wa_raw = reuse.tile([P, 4, N], F32, name="wa_raw", align_bytes=64, offset=22 * KIB)
+        wa_raw = reuse.tile([P, 4, N], F32, name="wa_raw", align_bytes=256, offset=22 * KIB)
         nc.sync.dma_start(wr_raw[:], wr_words.rearrange("a p y -> p a y").bitcast(I32))
         nc.sync.dma_start(we0_raw, we[0:512, :].rearrange("(p j) r -> p j r", j=4))
         nc.sync.dma_start(we1_raw, we[512:1024, :].rearrange("(p j) r -> p j r", j=4))
 
-        damp = [keep.tile([P, 4, HALF], F32, name="damp%d" % b, align_bytes=64) for b in range(2)]
-        md1 = reuse.tile([P, 4, HALF], F32, name="md1", align_bytes=64, offset=22 * KIB)
+        damp = [keep.tile([P, 4, HALF], F32, name="damp%d" % b, align_bytes=256) for b in range(2)]
+        md1 = reuse.tile([P, 4, HALF], F32, name="md1", align_bytes=256, offset=22 * KIB)
         md = [slots[:, 2 * HALF : 6 * HALF].rearrange("p (t n) -> p t n", t=4), md1[:]]
-        we_bf = [keep.tile([P, 4, P, 4], BF16, name="we_bf%d" % a, tag="we_bf%d" % a, align_bytes=64) for a in range(PASSES)]
-        we_q = [keep.tile([P, H], U32, name="we_q%d" % a, align_bytes=64) for a in range(PASSES)]
-        we_s = [keep.tile([P, H], U8, name="we_s%d" % a, align_bytes=64) for a in range(PASSES)]
-        wa_q = keep.tile([P, N], U32, name="wa_q", tag="vq00", align_bytes=64)
-        wa_s = keep.tile([P, N], U8, name="wa_s", align_bytes=64)
-        h_bf = keep.tile([P, S, 4], BF16, name="h_bf", align_bytes=64)
-        h_q = keep.tile([P, S], U32, name="h_q", tag="vq10", align_bytes=64)
-        h_s = keep.tile([P, S], U8, name="h_s", align_bytes=64)
+        we_bf = [keep.tile([P, 4, P, 4], BF16, name="we_bf%d" % a, tag="we_bf%d" % a, align_bytes=256) for a in range(PASSES)]
+        we_q = [keep.tile([P, H], U32, name="we_q%d" % a, align_bytes=256) for a in range(PASSES)]
+        we_s = [keep.tile([P, H], U8, name="we_s%d" % a, align_bytes=256) for a in range(PASSES)]
+        wa_q = keep.tile([P, N], U32, name="wa_q", tag="vq00", align_bytes=256)
+        wa_s = keep.tile([P, N], U8, name="wa_s", align_bytes=256)
+        h_bf = keep.tile([P, S, 4], BF16, name="h_bf", align_bytes=256)
+        h_q = keep.tile([P, S], U32, name="h_q", tag="vq10", align_bytes=256)
+        h_s = keep.tile([P, S], U8, name="h_s", align_bytes=256)
         out_v = out.rearrange("(u p) j -> p u j", p=P)
 
-        wa_bf = keep.tile([P, N, 4], BF16, name="wa_bf", tag="we_bf1", align_bytes=64)
+        wa_bf = keep.tile([P, N, 4], BF16, name="wa_bf", tag="we_bf1", align_bytes=256)
 
         def load_wa():
             wa_rows = wa.rearrange("(g t i) n -> t g i n", t=4, i=4)
@@ -154,7 +154,7 @@ def tile_list_factor_risk_allocation_kernel(
                 in_=wr_raw[:].rearrange("p a (g t i) -> p a t g i", t=4, i=2),
             )
 
-        sq = [keep.tile([P, 4, HALF], F32, name="sq%d" % b, align_bytes=64) for b in range(2)]
+        sq = [keep.tile([P, 4, HALF], F32, name="sq%d" % b, align_bytes=256) for b in range(2)]
 
         def square(b, t):
             nc.scalar.activation(out=sq[b][:, t, :], in_=c_acc[b][t][:], func=ACT.Square)
@@ -179,7 +179,7 @@ def tile_list_factor_risk_allocation_kernel(
 
         def copy_m(b, t, bank):
             acc = m_sum(b, t, bank)
-            m_sb = work.tile([P, HALF], F32, name="m_sb", align_bytes=64)
+            m_sb = work.tile([P, HALF], F32, name="m_sb", align_bytes=256)
             nc.scalar.copy(out=m_sb[:], in_=acc[:])
             return m_sb
 
@@ -253,7 +253,7 @@ def tile_list_factor_risk_allocation_kernel(
             if into is not None:
                 copy(out=into, in_=acc[:])
                 return
-            res = work.tile([P, 2, width], F32, name="res", tag="res", bufs=7, align_bytes=64)
+            res = work.tile([P, 2, width], F32, name="res", tag="res", bufs=7, align_bytes=256)
             copy(out=res[:], in_=acc[:])
             nc.sync.dma_start(out_v[:, :, cols], res[:])
 
@@ -329,7 +329,7 @@ def tile_list_factor_risk_allocation_kernel(
         allocate(6, 1, 2)
         contribute(7, e7, TOK // 2, TOK // 2)
         quant_h(7, 0.5)
-        last = keep.tile([P, 2, TOK], F32, name="last", align_bytes=64)
+        last = keep.tile([P, 2, TOK], F32, name="last", align_bytes=256)
         allocate(7, 0.5, 3, nc.scalar.copy, last[:, :, 0 : TOK // 2])
         quant_h(7.5, 0.5)
         allocate(7.5, 0.5, 6, nc.vector.tensor_copy, last[:, :, TOK // 2 : TOK])

@@ -35,7 +35,6 @@ def tile_list_factor_risk_allocation_kernel(
         psum = ctx.enter_context(tc.psum_pool(name="psum", bufs=1))
 
         offsets = keep.tile([P, S // 16], U16, name="offsets")
-        nc.sync.dma_start(offsets[:], offs)
 
         warm = keep.tile([P, 2], F32, name="warm")
         nc.vector.memset(warm[:, 0:1], 1.0)
@@ -47,6 +46,7 @@ def tile_list_factor_risk_allocation_kernel(
         wsc_r = keep.tile([P, PASSES, H // 4], I32, name="wsc_r", align_bytes=256)
         wsc_v = keep.tile([32, H // 4], I32, name="wsc_v", align_bytes=256)
         nc.sync.dma_start(tsc[0:32, :], tab_scales.rearrange("a q t -> q a t").bitcast(I32))
+        nc.sync.dma_start(offsets[:], offs)
         nc.sync.dma_start(wsc_v[:], wv_scales.rearrange("a q y -> q a y").bitcast(I32))
 
         tab0 = reuse.tile([P, T], I32, name="tab0", align_bytes=256, offset=8 * KIB)
@@ -307,8 +307,7 @@ def tile_list_factor_risk_allocation_kernel(
         contribute(2, exposure(2, 2))
         contribute(3, exposure(3, 3))
         quant_wa()
-        quant_h(0, 2)
-        quant_h(2, 2)
+        quant_h(0, 4)
         forecast(1, 2, 1)
         forecast(1, 3, 5, 2)
         e4 = exposure(4, 2)

@@ -21,6 +21,7 @@ PASSES = 2
 HALF = 512
 TOK = 128
 KIB = 1024
+EARLY = 1280
 
 
 def tile_list_factor_risk_allocation_kernel(
@@ -49,11 +50,13 @@ def tile_list_factor_risk_allocation_kernel(
         nc.sync.dma_start(offsets[:], offs)
         nc.sync.dma_start(wsc_v[:], wv_scales.rearrange("a q y -> q a y").bitcast(I32))
 
+        wv0_raw = keep.tile([P, H], I32, name="wv0_raw", align_bytes=256)
+        nc.sync.dma_start(wv0_raw[:], wv_words[0].rearrange("p y i -> p (y i)").bitcast(I32))
         tab0 = reuse.tile([P, T], I32, name="tab0", align_bytes=256, offset=8 * KIB)
         nc.sync.dma_start(tab0[:], tab_words[0].rearrange("p t i -> p (t i)").bitcast(I32))
-        wv_both = keep.tile([P, PASSES, H], I32, name="wv_both", align_bytes=256)
-        nc.sync.dma_start(wv_both[:], wv_words.rearrange("a p y i -> p a (y i)").bitcast(I32))
-        wv_raw = (wv_both[:, 0, :], wv_both[:, 1, :])
+        tab1 = keep.tile([P, T], I32, name="tab1", align_bytes=256)
+        tab1_words = tab_words[1].rearrange("p t i -> p (t i)").bitcast(I32)
+        nc.sync.dma_start(tab1[:, 0:EARLY], tab1_words[:, 0:EARLY])
 
         PW = (S + H) // 4
         planes = keep.tile([P, PASSES, PW], I32, name="planes", align_bytes=256)
@@ -77,8 +80,7 @@ def tile_list_factor_risk_allocation_kernel(
         nc.vector.tensor_copy(out=stage[:, 0 : S // 4], in_=sg[0:32, :].bitcast(I32))
         for q in (0, 2, 1, 3):
             nc.sync.dma_start(planes[32 * q : 32 * q + 4, :, :], stage[8 * q : 8 * q + 8, :])
-        tab1 = keep.tile([P, T], I32, name="tab1", tag="second", align_bytes=256)
-        nc.sync.dma_start(tab1[:], tab_words[1].rearrange("p t i -> p (t i)").bitcast(I32))
+        nc.sync.dma_start(tab1[:, EARLY:T], tab1_words[:, EARLY:T])
 
         planes8 = planes[:].bitcast(U8)
 
@@ -100,10 +102,10 @@ def tile_list_factor_risk_allocation_kernel(
         wv_q = [keep.tile([P, H], I32, name="wv_q%d" % a, align_bytes=256) for a in range(PASSES)]
         wr_q = keep.tile([P, PASSES, H // 2], I32, name="wr_q", align_bytes=256)
 
-        def permute_wv(a):
-            nc.vector.tensor_copy(
+        def permute_wv(a, raw, engine):
+            engine.tensor_copy(
                 out=wv_q[a][:].rearrange("p (t g i) -> p t g i", t=4, i=4),
-                in_=wv_raw[a].rearrange("p (g t i) -> p t g i", t=4, i=4),
+                in_=raw[:].rearrange("p (g t i) -> p t g i", t=4, i=4),
             )
 
         c_acc = [[psum.tile([P, HALF], F32, name="c%d%d" % (b, t), tag="bank%d" % (4 * b + t)) for t in range(4)] for b in range(2)]
@@ -116,16 +118,18 @@ def tile_list_factor_risk_allocation_kernel(
 
         gather(0, 0)
         gather(0, 1)
-        permute_wv(0)
-        permute_wv(1)
+        permute_wv(0, wv0_raw, nc.vector)
 
+        wv1_raw = reuse.tile([P, H], I32, name="wv1_raw", align_bytes=256, offset=18 * KIB)
         wr_raw = reuse.tile([P, PASSES, H // 2], I32, name="wr_raw", align_bytes=256, offset=20 * KIB)
-        slots = reuse.tile([P, 8 * HALF], F32, name="slots", align_bytes=256, offset=4 * KIB)
-        we0_raw, we1_raw = [slots[:, lo * HALF : (lo + 4) * HALF].rearrange("p (j r) -> p j r", j=4) for lo in (0, 4)]
-        we_raw = (we0_raw, we1_raw)
+        slots = reuse.tile([P, 8 * HALF], F32, name="slots", align_bytes=256, offset=2 * KIB)
+        we0_raw = [slots[:, lo * HALF : (lo + 2) * HALF].rearrange("p (j r) -> p j r", j=4) for lo in (0, 2)]
+        we1_raw = slots[:, 4 * HALF : 8 * HALF].rearrange("p (j r) -> p j r", j=4)
         wa_raw = reuse.tile([P, 4, N], F32, name="wa_raw", align_bytes=256, offset=22 * KIB)
+        nc.sync.dma_start(wv1_raw[:], wv_words[1].rearrange("p y i -> p (y i)").bitcast(I32))
+        nc.sync.dma_start(we0_raw[0], we[0:512, 0 : H // 2].rearrange("(p j) r -> p j r", j=4))
         nc.sync.dma_start(wr_raw[:], wr_words.rearrange("a p y -> p a y").bitcast(I32))
-        nc.sync.dma_start(we0_raw, we[0:512, :].rearrange("(p j) r -> p j r", j=4))
+        nc.sync.dma_start(we0_raw[1], we[0:512, H // 2 : H].rearrange("(p j) r -> p j r", j=4))
         nc.sync.dma_start(we1_raw, we[512:1024, :].rearrange("(p j) r -> p j r", j=4))
 
         damp = [keep.tile([P, 4, HALF], F32, name="damp%d" % b, align_bytes=256) for b in range(2)]
@@ -186,13 +190,10 @@ def tile_list_factor_risk_allocation_kernel(
         def forecast_gpsimd(b, t, m_sb):
             nc.gpsimd.tensor_tensor(out=md[b][:, t, :], in0=m_sb[:], in1=damp[b][:, t, :], op=ALU.mult)
 
-        def we_views(a, slots):
-            dst = we_bf[a][:, slots].rearrange("p t (g i) j -> p t g j i", i=4)
-            src = we_raw[a].rearrange("p j (g t i) -> p t g j i", t=4, i=4)[:, slots]
-            return dst, src
-
-        def round_we_vector(a, lo, hi):
-            dst, src = we_views(a, slice(lo, hi))
+        def round_we(a, raw, first, lo, hi):
+            count = raw.shape[2] // 4
+            dst = we_bf[a][:, lo:hi, first : first + count, :].rearrange("p t (g i) j -> p t g j i", i=4)
+            src = raw.rearrange("p j (g t i) -> p t g j i", t=4, i=4)[:, lo:hi]
             nc.vector.tensor_copy(out=dst, in_=src)
 
         def quant_we(a, lo=0, hi=4):
@@ -240,7 +241,9 @@ def tile_list_factor_risk_allocation_kernel(
                 in_=h_bf[:, cols, :].rearrange("p n t -> p (n t)"),
             )
 
-        def allocate(first, count, bank, copy=nc.scalar.copy, into=None):
+        res = keep.tile([P, 2, S], F32, name="res", align_bytes=256)
+
+        def allocate(first, count, bank, copy=nc.scalar.copy):
             cols = slice(int(TOK * first), int(TOK * (first + count)))
             width = int(TOK * count)
             acc = psum.tile([P, 2, width], F32, name="o%d" % first, tag="bank%d" % bank)
@@ -250,18 +253,18 @@ def tile_list_factor_risk_allocation_kernel(
                     lhsT_scale=wa_s[:, P * u : P * (u + 1)],
                     rhs=h_q[:, cols].bitcast(FP8X4), rhs_scale=h_s[:, cols], start=True, stop=True,
                 )
-            if into is not None:
-                copy(out=into, in_=acc[:])
-                return
-            res = work.tile([P, 2, width], F32, name="res", tag="res", bufs=7, align_bytes=256)
-            copy(out=res[:], in_=acc[:])
-            nc.sync.dma_start(out_v[:, :, cols], res[:])
+            copy(out=res[:, :, cols], in_=acc[:])
+
+        def store(first, count):
+            cols = slice(TOK * first, TOK * (first + count))
+            nc.sync.dma_start(out_v[:, :, cols], res[:, :, cols])
 
         for b in range(2):
             for t in range(4):
                 c_pass(0, b, t)
         gather(1, 0)
         gather(1, 1)
+        permute_wv(1, wv1_raw, nc.gpsimd)
         for t in range(4):
             c_pass(1, 0, t)
         c_pass(1, 1, 0)
@@ -276,16 +279,17 @@ def tile_list_factor_risk_allocation_kernel(
         square(1, 0)
         square(1, 1)
         root(0, 3)
+        round_we(0, we0_raw[0], 0, 0, 4)
         permute_wr()
-        round_we_vector(0, 0, 2)
-        round_we_vector(0, 2, 4)
+        round_we(0, we0_raw[1], P // 2, 0, 2)
+        round_we(0, we0_raw[1], P // 2, 2, 4)
         load_wa()
         quant_we(0, 0, 2)
         forecast(0, 0, 0)
         quant_we(0, 2, 4)
         forecast(0, 1, 1)
-        round_we_vector(1, 2, 4)
-        round_we_vector(1, 0, 2)
+        round_we(1, we1_raw, 0, 2, 4)
+        round_we(1, we1_raw, 0, 0, 2)
         quant_we(1, 2, 4)
         quant_we(1, 0, 2)
         c_pass(1, 1, 2)
@@ -315,6 +319,7 @@ def tile_list_factor_risk_allocation_kernel(
         contribute(4, e4)
         e5 = exposure(5, 3)
         allocate(2, 2, 7)
+        store(0, 4)
         contribute(5, e5)
         quant_h(4, 1)
         e6 = exposure(6, 1)
@@ -323,13 +328,14 @@ def tile_list_factor_risk_allocation_kernel(
         quant_h(5, 1)
         e7 = exposure(7, 5)
         allocate(5, 1, 4)
+        store(4, 2)
         contribute(7, e7, 0, TOK // 2)
         quant_h(6, 1)
         allocate(6, 1, 2)
+        store(6, 1)
         contribute(7, e7, TOK // 2, TOK // 2)
         quant_h(7, 0.5)
-        last = keep.tile([P, 2, TOK], F32, name="last", align_bytes=256)
-        allocate(7, 0.5, 3, nc.scalar.copy, last[:, :, 0 : TOK // 2])
+        allocate(7, 0.5, 3)
         quant_h(7.5, 0.5)
-        allocate(7.5, 0.5, 6, nc.vector.tensor_copy, last[:, :, TOK // 2 : TOK])
-        nc.sync.dma_start(out_v[:, :, S - TOK : S], last[:])
+        allocate(7.5, 0.5, 6, nc.vector.tensor_copy)
+        store(7, 1)

@@ -21,6 +21,8 @@ PASSES = 2
 HALF = 512
 TOK = 128
 KIB = 1024
+SHARE = 256
+FIRST = 320
 EARLY = 1280
 
 
@@ -123,17 +125,17 @@ def tile_list_factor_risk_allocation_kernel(
         wv1_raw = reuse.tile([P, H], I32, name="wv1_raw", align_bytes=256, offset=18 * KIB)
         wr_raw = reuse.tile([P, PASSES, H // 2], I32, name="wr_raw", align_bytes=256, offset=20 * KIB)
         slots = reuse.tile([P, 8 * HALF], F32, name="slots", align_bytes=256, offset=2 * KIB)
-        we0_raw = [slots[:, lo * HALF : (lo + 2) * HALF].rearrange("p (j r) -> p j r", j=4) for lo in (0, 2)]
+        we0_raw = [slots[:, 4 * lo : 4 * hi].rearrange("p (j r) -> p j r", j=4) for lo, hi in ((0, FIRST), (FIRST, H))]
         we1_raw = slots[:, 4 * HALF : 8 * HALF].rearrange("p (j r) -> p j r", j=4)
         wa_raw = reuse.tile([P, 4, N], F32, name="wa_raw", align_bytes=256, offset=22 * KIB)
         nc.sync.dma_start(wv1_raw[:], wv_words[1].rearrange("p y i -> p (y i)").bitcast(I32))
-        nc.sync.dma_start(we0_raw[0], we[0:512, 0 : H // 2].rearrange("(p j) r -> p j r", j=4))
         nc.sync.dma_start(wr_raw[:], wr_words.rearrange("a p y -> p a y").bitcast(I32))
-        nc.sync.dma_start(we0_raw[1], we[0:512, H // 2 : H].rearrange("(p j) r -> p j r", j=4))
+        nc.sync.dma_start(we0_raw[0], we[0:512, 0:FIRST].rearrange("(p j) r -> p j r", j=4))
+        nc.sync.dma_start(we0_raw[1], we[0:512, FIRST:H].rearrange("(p j) r -> p j r", j=4))
         nc.sync.dma_start(we1_raw, we[512:1024, :].rearrange("(p j) r -> p j r", j=4))
 
         damp = [keep.tile([P, 4, HALF], F32, name="damp%d" % b, align_bytes=256) for b in range(2)]
-        md1 = reuse.tile([P, 4, HALF], F32, name="md1", align_bytes=256, offset=22 * KIB)
+        md1 = keep.tile([P, 4, HALF], F32, name="md1", align_bytes=256)
         md = [slots[:, 2 * HALF : 6 * HALF].rearrange("p (t n) -> p t n", t=4), md1[:]]
         we_bf = [keep.tile([P, 4, P, 4], BF16, name="we_bf%d" % a, tag="we_bf%d" % a, align_bytes=256) for a in range(PASSES)]
         we_q = [keep.tile([P, H], U32, name="we_q%d" % a, align_bytes=256) for a in range(PASSES)]
@@ -145,7 +147,6 @@ def tile_list_factor_risk_allocation_kernel(
         h_s = keep.tile([P, S], U8, name="h_s", align_bytes=256)
         out_v = out.rearrange("(u p) j -> p u j", p=P)
 
-        wa_bf = keep.tile([P, N, 4], BF16, name="wa_bf", tag="we_bf1", align_bytes=256)
 
         def load_wa():
             wa_rows = wa.rearrange("(g t i) n -> t g i n", t=4, i=4)
@@ -153,18 +154,19 @@ def tile_list_factor_risk_allocation_kernel(
                 nc.sync.dma_start(wa_raw[:, t, :], wa_rows[t])
 
         def permute_wr():
-            nc.vector.tensor_copy(
+            nc.gpsimd.tensor_copy(
                 out=wr_q[:].rearrange("p a (t g i) -> p a t g i", t=4, i=2),
                 in_=wr_raw[:].rearrange("p a (g t i) -> p a t g i", t=4, i=2),
             )
 
-        sq = [keep.tile([P, 4, HALF], F32, name="sq%d" % b, align_bytes=256) for b in range(2)]
+        sq = [[keep.tile([P, HALF], F32, name="sq%d%d" % (b, t), tag="sq%d%d" % (b, t), align_bytes=256) for t in range(4)] for b in range(2)]
+        wa_bf = [keep.tile([P, P, 4], BF16, name="wa_bf%d" % u, tag=tag, align_bytes=256) for u, tag in enumerate(("we_bf1", "sq13"))]
 
         def square(b, t):
-            nc.scalar.activation(out=sq[b][:, t, :], in_=c_acc[b][t][:], func=ACT.Square)
+            nc.scalar.activation(out=sq[b][t][:], in_=c_acc[b][t][:], func=ACT.Square)
 
         def root(b, t, cols=slice(0, HALF)):
-            nc.scalar.activation(out=damp[b][:, t, cols], in_=sq[b][:, t, cols], func=ACT.Abs_reciprocal_sqrt, bias=1.0)
+            nc.scalar.activation(out=damp[b][:, t, cols], in_=sq[b][t][:, cols], func=ACT.Abs_reciprocal_sqrt, bias=1.0)
 
         def m_sum(b, t, bank):
             acc = psum.tile([P, HALF], F32, name="m%d%d" % (b, t), tag="bank%d" % bank)
@@ -175,20 +177,18 @@ def tile_list_factor_risk_allocation_kernel(
                 )
             return acc
 
+        def damp_m(b, t, acc, cols=slice(0, HALF)):
+            nc.vector.tensor_tensor(out=md[b][:, t, cols], in0=acc[:, cols], in1=damp[b][:, t, cols], op=ALU.mult)
+
         def forecast(b, t, bank, parts=1):
             acc = m_sum(b, t, bank)
             for i in range(parts):
-                cols = slice(HALF // parts * i, HALF // parts * (i + 1))
-                nc.vector.tensor_tensor(out=md[b][:, t, cols], in0=acc[:, cols], in1=damp[b][:, t, cols], op=ALU.mult)
+                damp_m(b, t, acc, slice(HALF // parts * i, HALF // parts * (i + 1)))
 
-        def copy_m(b, t, bank):
-            acc = m_sum(b, t, bank)
+        def damp_m_aside(b, t, acc, cols=slice(0, HALF)):
             m_sb = work.tile([P, HALF], F32, name="m_sb", align_bytes=256)
-            nc.scalar.copy(out=m_sb[:], in_=acc[:])
-            return m_sb
-
-        def forecast_gpsimd(b, t, m_sb):
-            nc.gpsimd.tensor_tensor(out=md[b][:, t, :], in0=m_sb[:], in1=damp[b][:, t, :], op=ALU.mult)
+            nc.scalar.copy(out=m_sb[:, cols], in_=acc[:, cols])
+            nc.gpsimd.tensor_tensor(out=md[b][:, t, cols], in0=m_sb[:, cols], in1=damp[b][:, t, cols], op=ALU.mult)
 
         def round_we(a, raw, first, lo, hi):
             count = raw.shape[2] // 4
@@ -205,24 +205,34 @@ def tile_list_factor_risk_allocation_kernel(
 
         def round_wa_gpsimd():
             nc.gpsimd.tensor_scalar(
-                out=wa_bf[:], in0=wa_raw[:].rearrange("p t n -> p n t"),
+                out=wa_bf[0][:], in0=wa_raw[:, :, 0:P].rearrange("p t n -> p n t"),
                 scalar1=1.0, scalar2=0.0, op0=ALU.mult, op1=ALU.add,
             )
 
-        def quant_wa():
-            nc.vector.quantize_mx(out=wa_q[:].bitcast(FP8X4), scales=wa_s[:], in_=wa_bf[:].rearrange("p n t -> p (n t)"))
+        def round_wa_scalar():
+            nc.scalar.copy(
+                out=wa_bf[1][:].rearrange("p (c i) t -> p c t i", i=4),
+                in_=wa_raw[:, :, P:N].rearrange("p t (c i) -> p c t i", i=4),
+            )
 
-        def exposure(s, bank):
+        def quant_wa(u):
+            cols = slice(P * u, P * (u + 1))
+            nc.vector.quantize_mx(out=wa_q[:, cols].bitcast(FP8X4), scales=wa_s[:, cols], in_=wa_bf[u][:].rearrange("p n t -> p (n t)"))
+
+        def exposure(s, bank, early=False):
             b, lo = divmod(TOK * s, HALF)
             acc = psum.tile([P, 4, TOK], F32, name="e%d" % s, tag="bank%d" % bank)
-            for t in (2, 3, 0, 1):
-                for a in (1, 0):
-                    nc.tensor.matmul_mx(
-                        out=acc[:, t, :], lhsT=we_q[a][:, P * t : P * (t + 1)].bitcast(FP8X4),
-                        lhsT_scale=we_s[a][:, P * t : P * (t + 1)],
-                        rhs=vq[a][b][:, lo : lo + TOK].bitcast(FP8X4), rhs_scale=v_scale(a, TOK * s, TOK),
-                        start=(a == 1), stop=(a == 0),
-                    )
+            if early:
+                steps = [(t, a, (a, t) == (0, 2), (a, t) == (1, 1)) for a in (0, 1) for t in (2, 3, 0, 1)]
+            else:
+                steps = [(t, a, a == 1, a == 0) for t in (2, 3, 0, 1) for a in (1, 0)]
+            for t, a, start, stop in steps:
+                nc.tensor.matmul_mx(
+                    out=acc[:, t, :], lhsT=we_q[a][:, P * t : P * (t + 1)].bitcast(FP8X4),
+                    lhsT_scale=we_s[a][:, P * t : P * (t + 1)],
+                    rhs=vq[a][b][:, lo : lo + TOK].bitcast(FP8X4), rhs_scale=v_scale(a, TOK * s, TOK),
+                    start=start, stop=stop,
+                )
             return acc
 
         def contribute(s, acc, first=0, count=TOK):
@@ -255,6 +265,14 @@ def tile_list_factor_risk_allocation_kernel(
                 )
             copy(out=res[:, :, cols], in_=acc[:])
 
+        def allocate_half(u, bank):
+            acc = psum.tile([P, HALF], F32, name="oh%d" % u, tag="bank%d" % bank)
+            nc.tensor.matmul_mx(
+                out=acc[:], lhsT=wa_q[:, P * u : P * (u + 1)].bitcast(FP8X4), lhsT_scale=wa_s[:, P * u : P * (u + 1)],
+                rhs=h_q[:, 0:HALF].bitcast(FP8X4), rhs_scale=h_s[:, 0:HALF], start=True, stop=True,
+            )
+            nc.scalar.copy(out=res[:, u, 0:HALF], in_=acc[:])
+
         def store(first, count):
             cols = slice(TOK * first, TOK * (first + count))
             nc.sync.dma_start(out_v[:, :, cols], res[:, :, cols])
@@ -265,6 +283,7 @@ def tile_list_factor_risk_allocation_kernel(
         gather(1, 0)
         gather(1, 1)
         permute_wv(1, wv1_raw, nc.gpsimd)
+        permute_wr()
         for t in range(4):
             c_pass(1, 0, t)
         c_pass(1, 1, 0)
@@ -280,9 +299,8 @@ def tile_list_factor_risk_allocation_kernel(
         square(1, 1)
         root(0, 3)
         round_we(0, we0_raw[0], 0, 0, 4)
-        permute_wr()
-        round_we(0, we0_raw[1], P // 2, 0, 2)
-        round_we(0, we0_raw[1], P // 2, 2, 4)
+        round_we(0, we0_raw[1], FIRST // 4, 0, 2)
+        round_we(0, we0_raw[1], FIRST // 4, 2, 4)
         load_wa()
         quant_we(0, 0, 2)
         forecast(0, 0, 0)
@@ -298,40 +316,44 @@ def tile_list_factor_risk_allocation_kernel(
         forecast(0, 3, 3, 2)
         round_wa_gpsimd()
         root(1, 0)
-        forecast_gpsimd(1, 0, copy_m(1, 0, 0))
+        damp_m_aside(1, 0, m_sum(1, 0, 0))
         root(1, 1)
-        forecast_gpsimd(1, 1, copy_m(1, 1, 4))
+        m11 = m_sum(1, 1, 4)
+        damp_m_aside(1, 1, m11, slice(SHARE, HALF))
         square(1, 2)
         square(1, 3)
         root(1, 2)
         root(1, 3, slice(0, 256))
         root(1, 3, slice(256, 512))
-        contribute(0, exposure(0, 1))
+        round_wa_scalar()
+        contribute(0, exposure(0, 1, True))
         contribute(1, exposure(1, 5))
         contribute(2, exposure(2, 2))
         contribute(3, exposure(3, 3))
-        quant_wa()
+        damp_m(1, 1, m11, slice(0, SHARE))
+        quant_wa(0)
         quant_h(0, 4)
+        allocate_half(0, 6)
         forecast(1, 2, 1)
         forecast(1, 3, 5, 2)
+        quant_wa(1)
+        allocate_half(1, 7)
+        store(0, 4)
         e4 = exposure(4, 2)
-        allocate(0, 2, 6)
         contribute(4, e4)
         e5 = exposure(5, 3)
-        allocate(2, 2, 7)
-        store(0, 4)
         contribute(5, e5)
         quant_h(4, 1)
-        e6 = exposure(6, 1)
-        allocate(4, 1, 0)
+        e6 = exposure(6, 0)
+        allocate(4, 1, 1)
         contribute(6, e6)
         quant_h(5, 1)
-        e7 = exposure(7, 5)
-        allocate(5, 1, 4)
+        e7 = exposure(7, 2)
+        allocate(5, 1, 5)
         store(4, 2)
         contribute(7, e7, 0, TOK // 2)
         quant_h(6, 1)
-        allocate(6, 1, 2)
+        allocate(6, 1, 4)
         store(6, 1)
         contribute(7, e7, TOK // 2, TOK // 2)
         quant_h(7, 0.5)

@@ -20,10 +20,9 @@ P = 128
 PASSES = 2
 HALF = 512
 TOK = 128
-KIB = 1024
 SHARE = 256
-FIRST = 320
-EARLY = 1280
+FIRST = 256
+EARLY = 1536
 
 
 def tile_list_factor_risk_allocation_kernel(
@@ -33,7 +32,6 @@ def tile_list_factor_risk_allocation_kernel(
 
     with ExitStack() as ctx:
         keep = ctx.enter_context(tc.tile_pool(name="keep", bufs=1))
-        reuse = ctx.enter_context(tc.tile_pool(name="reuse", bufs=1))
         work = ctx.enter_context(tc.tile_pool(name="work", bufs=3))
         psum = ctx.enter_context(tc.psum_pool(name="psum", bufs=1))
 
@@ -54,7 +52,7 @@ def tile_list_factor_risk_allocation_kernel(
 
         wv0_raw = keep.tile([P, H], I32, name="wv0_raw", align_bytes=256)
         nc.sync.dma_start(wv0_raw[:], wv_words[0].rearrange("p y i -> p (y i)").bitcast(I32))
-        tab0 = reuse.tile([P, T], I32, name="tab0", align_bytes=256, offset=8 * KIB)
+        tab0 = keep.tile([P, T], I32, name="tab0", align_bytes=256)
         nc.sync.dma_start(tab0[:], tab_words[0].rearrange("p t i -> p (t i)").bitcast(I32))
         tab1 = keep.tile([P, T], I32, name="tab1", align_bytes=256)
         tab1_words = tab_words[1].rearrange("p t i -> p (t i)").bitcast(I32)
@@ -62,7 +60,7 @@ def tile_list_factor_risk_allocation_kernel(
 
         PW = (S + H) // 4
         planes = keep.tile([P, PASSES, PW], I32, name="planes", align_bytes=256)
-        nc.gpsimd.memset(planes[:], 0)
+        nc.vector.memset(planes[:], 0)
         nc.gpsimd.memset(wsc_r[:], 0)
         for q in (0, 2, 1, 3):
             rows = wr_scales[:, 4 * q : 4 * q + 4, :].rearrange("a r y -> r a y").bitcast(I32)
@@ -104,10 +102,10 @@ def tile_list_factor_risk_allocation_kernel(
         wv_q = [keep.tile([P, H], I32, name="wv_q%d" % a, align_bytes=256) for a in range(PASSES)]
         wr_q = keep.tile([P, PASSES, H // 2], I32, name="wr_q", align_bytes=256)
 
-        def permute_wv(a, raw, engine):
+        def permute_wv(a, raw, engine, lo=0, hi=4):
             engine.tensor_copy(
-                out=wv_q[a][:].rearrange("p (t g i) -> p t g i", t=4, i=4),
-                in_=raw[:].rearrange("p (g t i) -> p t g i", t=4, i=4),
+                out=wv_q[a][:].rearrange("p (t g i) -> p t g i", t=4, i=4)[:, lo:hi],
+                in_=raw[:].rearrange("p (g t i) -> p t g i", t=4, i=4)[:, lo:hi],
             )
 
         c_acc = [[psum.tile([P, HALF], F32, name="c%d%d" % (b, t), tag="bank%d" % (4 * b + t)) for t in range(4)] for b in range(2)]
@@ -122,12 +120,12 @@ def tile_list_factor_risk_allocation_kernel(
         gather(0, 1)
         permute_wv(0, wv0_raw, nc.vector)
 
-        wv1_raw = reuse.tile([P, H], I32, name="wv1_raw", align_bytes=256, offset=18 * KIB)
-        wr_raw = reuse.tile([P, PASSES, H // 2], I32, name="wr_raw", align_bytes=256, offset=20 * KIB)
-        slots = reuse.tile([P, 8 * HALF], F32, name="slots", align_bytes=256, offset=2 * KIB)
+        wv1_raw = keep.tile([P, H], I32, name="wv1_raw", align_bytes=256)
+        wr_raw = keep.tile([P, PASSES, H // 2], I32, name="wr_raw", align_bytes=256)
+        slots = keep.tile([P, 8 * HALF], F32, name="slots", align_bytes=256)
         we0_raw = [slots[:, 4 * lo : 4 * hi].rearrange("p (j r) -> p j r", j=4) for lo, hi in ((0, FIRST), (FIRST, H))]
         we1_raw = slots[:, 4 * HALF : 8 * HALF].rearrange("p (j r) -> p j r", j=4)
-        wa_raw = reuse.tile([P, 4, N], F32, name="wa_raw", align_bytes=256, offset=22 * KIB)
+        wa_raw = keep.tile([P, 4, N], F32, name="wa_raw", align_bytes=256)
         nc.sync.dma_start(wv1_raw[:], wv_words[1].rearrange("p y i -> p (y i)").bitcast(I32))
         nc.sync.dma_start(wr_raw[:], wr_words.rearrange("a p y -> p a y").bitcast(I32))
         nc.sync.dma_start(we0_raw[0], we[0:512, 0:FIRST].rearrange("(p j) r -> p j r", j=4))
@@ -282,7 +280,8 @@ def tile_list_factor_risk_allocation_kernel(
                 c_pass(0, b, t)
         gather(1, 0)
         gather(1, 1)
-        permute_wv(1, wv1_raw, nc.gpsimd)
+        permute_wv(1, wv1_raw, nc.gpsimd, 0, 2)
+        permute_wv(1, wv1_raw, nc.gpsimd, 2, 4)
         permute_wr()
         for t in range(4):
             c_pass(1, 0, t)
@@ -296,15 +295,15 @@ def tile_list_factor_risk_allocation_kernel(
         square(0, 3)
         root(0, 2)
         square(1, 0)
-        square(1, 1)
         root(0, 3)
+        square(1, 1)
         round_we(0, we0_raw[0], 0, 0, 4)
         round_we(0, we0_raw[1], FIRST // 4, 0, 2)
         round_we(0, we0_raw[1], FIRST // 4, 2, 4)
         load_wa()
         quant_we(0, 0, 2)
-        forecast(0, 0, 0)
         quant_we(0, 2, 4)
+        forecast(0, 0, 0)
         forecast(0, 1, 1)
         round_we(1, we1_raw, 0, 2, 4)
         round_we(1, we1_raw, 0, 0, 2)
@@ -333,18 +332,18 @@ def tile_list_factor_risk_allocation_kernel(
         damp_m(1, 1, m11, slice(0, SHARE))
         quant_wa(0)
         quant_h(0, 4)
-        allocate_half(0, 6)
+        allocate_half(0, 0)
         forecast(1, 2, 1)
         forecast(1, 3, 5, 2)
         quant_wa(1)
-        allocate_half(1, 7)
+        allocate_half(1, 6)
         store(0, 4)
         e4 = exposure(4, 2)
         contribute(4, e4)
         e5 = exposure(5, 3)
         contribute(5, e5)
         quant_h(4, 1)
-        e6 = exposure(6, 0)
+        e6 = exposure(6, 7)
         allocate(4, 1, 1)
         contribute(6, e6)
         quant_h(5, 1)
@@ -359,5 +358,5 @@ def tile_list_factor_risk_allocation_kernel(
         quant_h(7, 0.5)
         allocate(7, 0.5, 3)
         quant_h(7.5, 0.5)
-        allocate(7.5, 0.5, 6, nc.vector.tensor_copy)
+        allocate(7.5, 0.5, 0, nc.vector.tensor_copy)
         store(7, 1)

@@ -18,11 +18,12 @@ ALU = mybir.AluOpType
 
 P = 128
 PASSES = 2
-HALF = 512
+BANK = 512
+QUART = 256
 TOK = 128
-SHARE = 256
-FIRST = 256
 EARLY = 1536
+ASIDE = (4, 5, 6)
+SHARE = 256
 
 
 def tile_list_factor_risk_allocation_kernel(
@@ -32,7 +33,6 @@ def tile_list_factor_risk_allocation_kernel(
 
     with ExitStack() as ctx:
         keep = ctx.enter_context(tc.tile_pool(name="keep", bufs=1))
-        work = ctx.enter_context(tc.tile_pool(name="work", bufs=3))
         psum = ctx.enter_context(tc.psum_pool(name="psum", bufs=1))
 
         offsets = keep.tile([P, S // 16], U16, name="offsets")
@@ -42,16 +42,16 @@ def tile_list_factor_risk_allocation_kernel(
         nc.scalar.activation(out=warm[:, 1:2], in_=warm[:, 0:1], func=ACT.Abs_reciprocal_sqrt)
 
         tsc = keep.tile([P, T // 4], I32, name="tsc", align_bytes=256)
+        wsc_v = keep.tile([32, H // 4], I32, name="wsc_v", align_bytes=256)
+        wsc_r = keep.tile([P, PASSES, H // 4], I32, name="wsc_r", align_bytes=256)
         nc.vector.memset(tsc[32:64, :], 0)
         nc.vector.memset(tsc[64:128, :], 0)
-        wsc_r = keep.tile([P, PASSES, H // 4], I32, name="wsc_r", align_bytes=256)
-        wsc_v = keep.tile([32, H // 4], I32, name="wsc_v", align_bytes=256)
         nc.sync.dma_start(tsc[0:32, :], tab_scales.rearrange("a q t -> q a t").bitcast(I32))
         nc.sync.dma_start(offsets[:], offs)
         nc.sync.dma_start(wsc_v[:], wv_scales.rearrange("a q y -> q a y").bitcast(I32))
 
-        wv0_raw = keep.tile([P, H], I32, name="wv0_raw", align_bytes=256)
-        nc.sync.dma_start(wv0_raw[:], wv_words[0].rearrange("p y i -> p (y i)").bitcast(I32))
+        wv_raw = [keep.tile([P, H], I32, name="wv_raw%d" % a, align_bytes=256) for a in range(PASSES)]
+        nc.sync.dma_start(wv_raw[0][:], wv_words[0].rearrange("p y i -> p (y i)").bitcast(I32))
         tab0 = keep.tile([P, T], I32, name="tab0", align_bytes=256)
         nc.sync.dma_start(tab0[:], tab_words[0].rearrange("p t i -> p (t i)").bitcast(I32))
         tab1 = keep.tile([P, T], I32, name="tab1", align_bytes=256)
@@ -69,19 +69,17 @@ def tile_list_factor_risk_allocation_kernel(
         nc.gpsimd.tensor_copy(
             out=wr_s[:].rearrange("p a (t g) -> p a t g", t=4), in_=wsc_r[:].rearrange("p a (g t) -> p a t g", t=4)
         )
-        sg = keep.tile([P, S], U8, name="sg", tag="second", align_bytes=256)
+        sg = keep.tile([P, S], U8, name="sg", align_bytes=256)
         nc.vector.tensor_copy(sg[:], tsc[:].bitcast(U8).indirect(offsets[:]))
-        stage = keep.tile([32, PW], I32, name="stage", tag="third", align_bytes=256)
-        for src, lo in ((wsc_v, S // 4),):
-            nc.vector.tensor_copy(
-                out=stage[:, lo : lo + H // 4].rearrange("p (t c k) -> p c t k", t=4, k=4),
-                in_=src[:].rearrange("p (c k t) -> p c t k", t=4, k=4),
-            )
+        stage = keep.tile([32, PW], I32, name="stage", align_bytes=256)
+        nc.vector.tensor_copy(
+            out=stage[:, S // 4 : PW].rearrange("p (t c k) -> p c t k", t=4, k=4),
+            in_=wsc_v[:].rearrange("p (c k t) -> p c t k", t=4, k=4),
+        )
         nc.vector.tensor_copy(out=stage[:, 0 : S // 4], in_=sg[0:32, :].bitcast(I32))
         for q in (0, 2, 1, 3):
             nc.sync.dma_start(planes[32 * q : 32 * q + 4, :, :], stage[8 * q : 8 * q + 8, :])
         nc.sync.dma_start(tab1[:, EARLY:T], tab1_words[:, EARLY:T])
-
         planes8 = planes[:].bitcast(U8)
 
         def v_scale(a, lo, n):
@@ -93,108 +91,114 @@ def tile_list_factor_risk_allocation_kernel(
         def wr_scale(a, t):
             return wr_s[:].bitcast(U8)[:, a, P * t : P * (t + 1)]
 
-        vq = [[keep.tile([P, HALF], U32, name="vq%d%d" % (a, b), tag="vq%d%d" % (a, b), align_bytes=256) for b in range(2)] for a in range(PASSES)]
+        vq = [keep.tile([P, S], U32, name="vq%d" % a, align_bytes=256) for a in range(PASSES)]
 
-        def gather(a, b):
+        def gather(a, lo, n):
             win = (tab0[:], tab1[:])[a]
-            nc.vector.tensor_copy(vq[a][b][:], win.bitcast(U32).indirect(offsets[:, 32 * b : 32 * (b + 1)]))
+            nc.vector.tensor_copy(vq[a][:, lo : lo + n], win.bitcast(U32).indirect(offsets[:, lo // 16 : (lo + n) // 16]))
 
         wv_q = [keep.tile([P, H], I32, name="wv_q%d" % a, align_bytes=256) for a in range(PASSES)]
         wr_q = keep.tile([P, PASSES, H // 2], I32, name="wr_q", align_bytes=256)
 
-        def permute_wv(a, raw, engine, lo=0, hi=4):
-            engine.tensor_copy(
-                out=wv_q[a][:].rearrange("p (t g i) -> p t g i", t=4, i=4)[:, lo:hi],
-                in_=raw[:].rearrange("p (g t i) -> p t g i", t=4, i=4)[:, lo:hi],
+        def permute_wv(a, copy, dtype, lo, hi):
+            copy(
+                out=wv_q[a][:].bitcast(dtype).rearrange("p (t g i) -> p t g i", t=4, i=4)[:, lo:hi],
+                in_=wv_raw[a][:].bitcast(dtype).rearrange("p (g t i) -> p t g i", t=4, i=4)[:, lo:hi],
             )
 
-        c_acc = [[psum.tile([P, HALF], F32, name="c%d%d" % (b, t), tag="bank%d" % (4 * b + t)) for t in range(4)] for b in range(2)]
+        c_acc = [psum.tile([P, 2, QUART], F32, name="c%d" % k, tag="bank%d" % (k % 7)) for k in range(8)]
 
-        def c_pass(a, b, t):
-            nc.tensor.matmul_mx(
-                out=c_acc[b][t][:], lhsT=wv_q[a][:, P * t : P * (t + 1)].bitcast(FP8X4), lhsT_scale=wv_scale(a, t),
-                rhs=vq[a][b][:].bitcast(FP8X4), rhs_scale=v_scale(a, HALF * b, HALF), start=(a == 0), stop=(a == 1),
-            )
+        def c_pass(a, k):
+            q, h = divmod(k, 2)
+            for j in range(2):
+                t = 2 * h + j
+                nc.tensor.matmul_mx(
+                    out=c_acc[k][:, j, :], lhsT=wv_q[a][:, P * t : P * (t + 1)].bitcast(FP8X4), lhsT_scale=wv_scale(a, t),
+                    rhs=vq[a][:, QUART * q : QUART * (q + 1)].bitcast(FP8X4), rhs_scale=v_scale(a, QUART * q, QUART),
+                    start=(a, j) == (0, 0), stop=(a, j) == (1, 1),
+                )
 
-        gather(0, 0)
-        gather(0, 1)
-        permute_wv(0, wv0_raw, nc.vector)
+        gather(0, 0, BANK)
+        gather(0, BANK, BANK)
+        permute_wv(0, nc.vector.tensor_copy, I32, 0, 4)
 
-        wv1_raw = keep.tile([P, H], I32, name="wv1_raw", align_bytes=256)
         wr_raw = keep.tile([P, PASSES, H // 2], I32, name="wr_raw", align_bytes=256)
-        slots = keep.tile([P, 8 * HALF], F32, name="slots", align_bytes=256)
-        we0_raw = [slots[:, 4 * lo : 4 * hi].rearrange("p (j r) -> p j r", j=4) for lo, hi in ((0, FIRST), (FIRST, H))]
-        we1_raw = slots[:, 4 * HALF : 8 * HALF].rearrange("p (j r) -> p j r", j=4)
+        we_parts = ((0, 0, H // 2), (0, H // 2, H), (1, 0, H))
+        we_raw = [keep.tile([P, 4, hi - lo], F32, name="we_raw%d" % i, align_bytes=256) for i, (a, lo, hi) in enumerate(we_parts)]
         wa_raw = keep.tile([P, 4, N], F32, name="wa_raw", align_bytes=256)
-        nc.sync.dma_start(wv1_raw[:], wv_words[1].rearrange("p y i -> p (y i)").bitcast(I32))
+        nc.sync.dma_start(wv_raw[1][:], wv_words[1].rearrange("p y i -> p (y i)").bitcast(I32))
         nc.sync.dma_start(wr_raw[:], wr_words.rearrange("a p y -> p a y").bitcast(I32))
-        nc.sync.dma_start(we0_raw[0], we[0:512, 0:FIRST].rearrange("(p j) r -> p j r", j=4))
-        nc.sync.dma_start(we0_raw[1], we[0:512, FIRST:H].rearrange("(p j) r -> p j r", j=4))
-        nc.sync.dma_start(we1_raw, we[512:1024, :].rearrange("(p j) r -> p j r", j=4))
+        for raw, (a, lo, hi) in zip(we_raw, we_parts):
+            nc.sync.dma_start(raw[:], we[512 * a : 512 * (a + 1), lo:hi].rearrange("(p j) r -> p j r", j=4))
+        wa_rows = wa.rearrange("(g t i) n -> t g i n", t=4, i=4)
+        for t in range(4):
+            nc.sync.dma_start(wa_raw[:, t, :], wa_rows[t])
 
-        damp = [keep.tile([P, 4, HALF], F32, name="damp%d" % b, align_bytes=256) for b in range(2)]
-        md1 = keep.tile([P, 4, HALF], F32, name="md1", align_bytes=256)
-        md = [slots[:, 2 * HALF : 6 * HALF].rearrange("p (t n) -> p t n", t=4), md1[:]]
+        sq = [keep.tile([P, BANK], F32, name="sq%d" % k, tag="sq%d" % k, align_bytes=256) for k in range(8)]
+        damp = [[keep.tile([P, QUART], F32, name="damp%d%d" % (k, j), tag="damp%d%d" % (k, j), align_bytes=256) for j in range(2)] for k in range(1)]
+        damp = damp + [keep.tile([P, BANK], F32, name="damp%d" % k, tag="damp%d" % k, align_bytes=256) for k in range(1, 8)]
         we_bf = [keep.tile([P, 4, P, 4], BF16, name="we_bf%d" % a, tag="we_bf%d" % a, align_bytes=256) for a in range(PASSES)]
+        h_bf = [keep.tile([P, BANK, 4], BF16, name="h_bf%d" % b, tag="h_bf%d" % b, align_bytes=256) for b in range(2)]
+        md = [keep.tile([P, 4 * QUART], F32, name="md%d" % q, tag=tag, align_bytes=256)[:] for q, tag in enumerate(("md0", "md1", "md2", "h_bf0"))]
+        m_sb = {k: keep.tile([P, BANK], F32, name="m_sb%d" % k, tag="m_sb%d" % k, align_bytes=256) for k in ASIDE}
         we_q = [keep.tile([P, H], U32, name="we_q%d" % a, align_bytes=256) for a in range(PASSES)]
         we_s = [keep.tile([P, H], U8, name="we_s%d" % a, align_bytes=256) for a in range(PASSES)]
-        wa_q = keep.tile([P, N], U32, name="wa_q", tag="vq00", align_bytes=256)
+        wa_q = [keep.tile([P, P], U32, name="wa_q%d" % u, tag=tag, align_bytes=256) for u, tag in enumerate(("wa_q0", "damp6"))]
         wa_s = keep.tile([P, N], U8, name="wa_s", align_bytes=256)
-        h_bf = keep.tile([P, S, 4], BF16, name="h_bf", align_bytes=256)
-        h_q = keep.tile([P, S], U32, name="h_q", tag="vq10", align_bytes=256)
+        h_q = [keep.tile([P, BANK], U32, name="h_q%d" % b, tag=tag, align_bytes=256) for b, tag in enumerate(("h_q0", "m_sb6"))]
         h_s = keep.tile([P, S], U8, name="h_s", align_bytes=256)
+        wa_bf = [keep.tile([P, P, 4], BF16, name="wa_bf%d" % u, tag=tag, align_bytes=256) for u, tag in enumerate(("we_bf1", "sq7"))]
+        res = keep.tile([P, 2, S], F32, name="res", align_bytes=256)
         out_v = out.rearrange("(u p) j -> p u j", p=P)
 
-
-        def load_wa():
-            wa_rows = wa.rearrange("(g t i) n -> t g i n", t=4, i=4)
-            for t in range(4):
-                nc.sync.dma_start(wa_raw[:, t, :], wa_rows[t])
-
-        def permute_wr():
+        def permute_wr(lo, hi):
             nc.gpsimd.tensor_copy(
-                out=wr_q[:].rearrange("p a (t g i) -> p a t g i", t=4, i=2),
-                in_=wr_raw[:].rearrange("p a (g t i) -> p a t g i", t=4, i=2),
+                out=wr_q[:].rearrange("p a (t g i) -> p a t g i", t=4, i=2)[:, :, lo:hi],
+                in_=wr_raw[:].rearrange("p a (g t i) -> p a t g i", t=4, i=2)[:, :, lo:hi],
             )
 
-        sq = [[keep.tile([P, HALF], F32, name="sq%d%d" % (b, t), tag="sq%d%d" % (b, t), align_bytes=256) for t in range(4)] for b in range(2)]
-        wa_bf = [keep.tile([P, P, 4], BF16, name="wa_bf%d" % u, tag=tag, align_bytes=256) for u, tag in enumerate(("we_bf1", "sq13"))]
+        def flat(acc):
+            return acc[:].rearrange("p j n -> p (j n)")
 
-        def square(b, t):
-            nc.scalar.activation(out=sq[b][t][:], in_=c_acc[b][t][:], func=ACT.Square)
+        def square(k, cols=slice(0, BANK)):
+            nc.scalar.activation(out=sq[k][:, cols], in_=flat(c_acc[k])[:, cols], func=ACT.Square)
 
-        def root(b, t, cols=slice(0, HALF)):
-            nc.scalar.activation(out=damp[b][:, t, cols], in_=sq[b][t][:, cols], func=ACT.Abs_reciprocal_sqrt, bias=1.0)
+        def root(k, cols=slice(0, BANK)):
+            nc.scalar.activation(out=damp[k][:, cols], in_=sq[k][:, cols], func=ACT.Abs_reciprocal_sqrt, bias=1.0)
 
-        def m_sum(b, t, bank):
-            acc = psum.tile([P, HALF], F32, name="m%d%d" % (b, t), tag="bank%d" % bank)
-            for a in range(PASSES):
-                nc.tensor.matmul_mx(
-                    out=acc[:], lhsT=wr_q[:, a, 64 * t : 64 * (t + 1)].bitcast(U8).bitcast(FP4X4), lhsT_scale=wr_scale(a, t),
-                    rhs=vq[a][b][:].bitcast(FP8X4), rhs_scale=v_scale(a, HALF * b, HALF), start=(a == 0), stop=(a == 1),
-                )
+        def m_sum(k, bank):
+            q, h = divmod(k, 2)
+            acc = psum.tile([P, 2, QUART], F32, name="m%d" % k, tag="bank%d" % bank)
+            for j in range(2):
+                t = 2 * h + j
+                for a in range(PASSES):
+                    nc.tensor.matmul_mx(
+                        out=acc[:, j, :], lhsT=wr_q[:, a, 64 * t : 64 * (t + 1)].bitcast(U8).bitcast(FP4X4), lhsT_scale=wr_scale(a, t),
+                        rhs=vq[a][:, QUART * q : QUART * (q + 1)].bitcast(FP8X4), rhs_scale=v_scale(a, QUART * q, QUART),
+                        start=(a == 0), stop=(a == 1),
+                    )
             return acc
 
-        def damp_m(b, t, acc, cols=slice(0, HALF)):
-            nc.vector.tensor_tensor(out=md[b][:, t, cols], in0=acc[:, cols], in1=damp[b][:, t, cols], op=ALU.mult)
+        def md_of(k):
+            q, h = divmod(k, 2)
+            return md[q][:, BANK * h : BANK * (h + 1)]
 
-        def forecast(b, t, bank, parts=1):
-            acc = m_sum(b, t, bank)
-            for i in range(parts):
-                damp_m(b, t, acc, slice(HALF // parts * i, HALF // parts * (i + 1)))
+        def damp_m(k, acc, cols=slice(0, BANK)):
+            nc.vector.tensor_tensor(out=md_of(k)[:, cols], in0=flat(acc)[:, cols], in1=damp[k][:, cols], op=ALU.mult)
 
-        def damp_m_aside(b, t, acc, cols=slice(0, HALF)):
-            m_sb = work.tile([P, HALF], F32, name="m_sb", align_bytes=256)
-            nc.scalar.copy(out=m_sb[:, cols], in_=acc[:, cols])
-            nc.gpsimd.tensor_tensor(out=md[b][:, t, cols], in0=m_sb[:, cols], in1=damp[b][:, t, cols], op=ALU.mult)
+        def copy_m(k, acc, cols=slice(0, BANK)):
+            nc.scalar.copy(out=m_sb[k][:, cols], in_=flat(acc)[:, cols])
 
-        def round_we(a, raw, first, lo, hi):
-            count = raw.shape[2] // 4
-            dst = we_bf[a][:, lo:hi, first : first + count, :].rearrange("p t (g i) j -> p t g j i", i=4)
-            src = raw.rearrange("p j (g t i) -> p t g j i", t=4, i=4)[:, lo:hi]
+        def damp_m_aside(k, cols=slice(0, BANK)):
+            nc.gpsimd.tensor_tensor(out=md_of(k)[:, cols], in0=m_sb[k][:, cols], in1=damp[k][:, cols], op=ALU.mult)
+
+        def round_we(part, lo, hi):
+            a, first, last = we_parts[part]
+            dst = we_bf[a][:, lo:hi, first // 4 : last // 4, :].rearrange("p t (g i) j -> p t g j i", i=4)
+            src = we_raw[part][:].rearrange("p j (g t i) -> p t g j i", t=4, i=4)[:, lo:hi]
             nc.vector.tensor_copy(out=dst, in_=src)
 
-        def quant_we(a, lo=0, hi=4):
+        def quant_we(a, lo, hi):
             cols = slice(P * lo, P * hi)
             nc.vector.quantize_mx(
                 out=we_q[a][:, cols].bitcast(FP8X4), scales=we_s[a][:, cols],
@@ -215,148 +219,165 @@ def tile_list_factor_risk_allocation_kernel(
 
         def quant_wa(u):
             cols = slice(P * u, P * (u + 1))
-            nc.vector.quantize_mx(out=wa_q[:, cols].bitcast(FP8X4), scales=wa_s[:, cols], in_=wa_bf[u][:].rearrange("p n t -> p (n t)"))
+            nc.vector.quantize_mx(out=wa_q[u][:].bitcast(FP8X4), scales=wa_s[:, cols], in_=wa_bf[u][:].rearrange("p n t -> p (n t)"))
 
-        def exposure(s, bank, early=False):
-            b, lo = divmod(TOK * s, HALF)
-            acc = psum.tile([P, 4, TOK], F32, name="e%d" % s, tag="bank%d" % bank)
-            if early:
-                steps = [(t, a, (a, t) == (0, 2), (a, t) == (1, 1)) for a in (0, 1) for t in (2, 3, 0, 1)]
-            else:
-                steps = [(t, a, a == 1, a == 0) for t in (2, 3, 0, 1) for a in (1, 0)]
+        def e_tile(s, bank):
+            return psum.tile([P, 4, TOK], F32, name="e%d" % s, tag="bank%d" % bank)
+
+        def e_passes(s, acc, steps):
+            cols = slice(TOK * s, TOK * (s + 1))
             for t, a, start, stop in steps:
                 nc.tensor.matmul_mx(
                     out=acc[:, t, :], lhsT=we_q[a][:, P * t : P * (t + 1)].bitcast(FP8X4),
                     lhsT_scale=we_s[a][:, P * t : P * (t + 1)],
-                    rhs=vq[a][b][:, lo : lo + TOK].bitcast(FP8X4), rhs_scale=v_scale(a, TOK * s, TOK),
-                    start=start, stop=stop,
+                    rhs=vq[a][:, cols].bitcast(FP8X4), rhs_scale=v_scale(a, TOK * s, TOK), start=start, stop=stop,
                 )
+
+        def e_open(s, bank):
+            acc = e_tile(s, bank)
+            e_passes(s, acc, [(t, 0, t == 0, False) for t in range(4)])
+            return acc
+
+        def e_close(s, acc):
+            e_passes(s, acc, [(t, 1, False, t == 1) for t in (2, 3, 0, 1)])
+
+        def exposure(s, bank):
+            acc = e_tile(s, bank)
+            e_passes(s, acc, [(t, a, a == 1, a == 0) for t in (2, 3, 0, 1) for a in (1, 0)])
             return acc
 
         def contribute(s, acc, first=0, count=TOK):
-            b, lo = divmod(TOK * s + first, HALF)
+            q, lo = divmod(TOK * s + first, QUART)
+            b, at = divmod(TOK * s + first, BANK)
             nc.vector.tensor_tensor(
-                out=h_bf[:, HALF * b + lo : HALF * b + lo + count, :].rearrange("p (c i) t -> p c t i", i=4),
+                out=h_bf[b][:, at : at + count, :].rearrange("p (c i) t -> p c t i", i=4),
                 in0=acc[:, :, first : first + count].rearrange("p t (c i) -> p c t i", i=4),
-                in1=md[b][:, :, lo : lo + count].rearrange("p t (c i) -> p c t i", i=4),
+                in1=md[q].rearrange("p (t n) -> p t n", t=4)[:, :, lo : lo + count].rearrange("p t (c i) -> p c t i", i=4),
                 op=ALU.mult,
             )
 
         def quant_h(first, count):
-            cols = slice(int(TOK * first), int(TOK * (first + count)))
+            b, at = divmod(first, BANK)
             nc.vector.quantize_mx(
-                out=h_q[:, cols].bitcast(FP8X4), scales=h_s[:, cols],
-                in_=h_bf[:, cols, :].rearrange("p n t -> p (n t)"),
+                out=h_q[b][:, at : at + count].bitcast(FP8X4), scales=h_s[:, first : first + count],
+                in_=h_bf[b][:, at : at + count, :].rearrange("p n t -> p (n t)"),
             )
 
-        res = keep.tile([P, 2, S], F32, name="res", align_bytes=256)
-
-        def allocate(first, count, bank, copy=nc.scalar.copy):
-            cols = slice(int(TOK * first), int(TOK * (first + count)))
-            width = int(TOK * count)
-            acc = psum.tile([P, 2, width], F32, name="o%d" % first, tag="bank%d" % bank)
-            for u in range(2):
+        def allocate(first, count, bank, rows=(0, 1), copy=nc.scalar.copy):
+            cols = slice(first, first + count)
+            b, at = divmod(first, BANK)
+            acc = psum.tile([P, len(rows), count], F32, name="o%d_%d" % (first, rows[0]), tag="bank%d" % bank)
+            for j, u in enumerate(rows):
                 nc.tensor.matmul_mx(
-                    out=acc[:, u, :], lhsT=wa_q[:, P * u : P * (u + 1)].bitcast(FP8X4),
+                    out=acc[:, j, :], lhsT=wa_q[u][:].bitcast(FP8X4),
                     lhsT_scale=wa_s[:, P * u : P * (u + 1)],
-                    rhs=h_q[:, cols].bitcast(FP8X4), rhs_scale=h_s[:, cols], start=True, stop=True,
+                    rhs=h_q[b][:, at : at + count].bitcast(FP8X4), rhs_scale=h_s[:, cols], start=True, stop=True,
                 )
-            copy(out=res[:, :, cols], in_=acc[:])
+            copy(out=res[:, rows[0] : rows[-1] + 1, cols], in_=acc[:])
 
-        def allocate_half(u, bank):
-            acc = psum.tile([P, HALF], F32, name="oh%d" % u, tag="bank%d" % bank)
-            nc.tensor.matmul_mx(
-                out=acc[:], lhsT=wa_q[:, P * u : P * (u + 1)].bitcast(FP8X4), lhsT_scale=wa_s[:, P * u : P * (u + 1)],
-                rhs=h_q[:, 0:HALF].bitcast(FP8X4), rhs_scale=h_s[:, 0:HALF], start=True, stop=True,
-            )
-            nc.scalar.copy(out=res[:, u, 0:HALF], in_=acc[:])
+        def store(first, count, rows=slice(0, 2)):
+            cols = slice(first, first + count)
+            nc.sync.dma_start(out_v[:, rows, cols], res[:, rows, cols])
 
-        def store(first, count):
-            cols = slice(TOK * first, TOK * (first + count))
-            nc.sync.dma_start(out_v[:, :, cols], res[:, :, cols])
-
-        for b in range(2):
-            for t in range(4):
-                c_pass(0, b, t)
-        gather(1, 0)
-        gather(1, 1)
-        permute_wv(1, wv1_raw, nc.gpsimd, 0, 2)
-        permute_wv(1, wv1_raw, nc.gpsimd, 2, 4)
-        permute_wr()
-        for t in range(4):
-            c_pass(1, 0, t)
-        c_pass(1, 1, 0)
-        c_pass(1, 1, 1)
-        square(0, 0)
-        square(0, 1)
-        root(0, 0)
-        root(0, 1)
-        square(0, 2)
-        square(0, 3)
-        root(0, 2)
-        square(1, 0)
-        root(0, 3)
-        square(1, 1)
-        round_we(0, we0_raw[0], 0, 0, 4)
-        round_we(0, we0_raw[1], FIRST // 4, 0, 2)
-        round_we(0, we0_raw[1], FIRST // 4, 2, 4)
-        load_wa()
+        for k in range(7):
+            c_pass(0, k)
+        permute_wv(1, nc.scalar.copy, U32, 0, 2)
+        permute_wv(1, nc.scalar.copy, U32, 2, 4)
+        permute_wr(0, 2)
+        permute_wr(2, 4)
+        for q in range(4):
+            gather(1, QUART * q, QUART)
+        round_we(0, 0, 4)
+        c_pass(1, 0)
+        for j in range(2):
+            square(0, slice(QUART * j, QUART * (j + 1)))
+        for j in range(2):
+            nc.scalar.activation(out=damp[0][j][:], in_=sq[0][:, QUART * j : QUART * (j + 1)], func=ACT.Abs_reciprocal_sqrt, bias=1.0)
+        m0 = m_sum(0, 7)
+        for j in range(2):
+            nc.vector.tensor_tensor(out=md[0][:, QUART * j : QUART * (j + 1)], in0=m0[:, j, :], in1=damp[0][j][:], op=ALU.mult)
+        c_pass(1, 1)
+        c_pass(1, 2)
+        square(1)
+        m1 = m_sum(1, 1)
+        square(2)
+        m2 = m_sum(2, 2)
+        c_pass(1, 3)
+        root(1)
+        root(2)
+        round_we(1, 0, 2)
+        round_we(1, 2, 4)
         quant_we(0, 0, 2)
         quant_we(0, 2, 4)
-        forecast(0, 0, 0)
-        forecast(0, 1, 1)
-        round_we(1, we1_raw, 0, 2, 4)
-        round_we(1, we1_raw, 0, 0, 2)
+        damp_m(1, m1)
+        damp_m(2, m2)
+        for k in range(4, 7):
+            c_pass(1, k)
+        square(3)
+        m3 = m_sum(3, 3)
+        square(4)
+        square(5)
+        e0 = e_open(0, 7)
+        e1 = e_open(1, 1)
+        m4 = m_sum(4, 4)
+        m5 = m_sum(5, 5)
+        root(3)
+        round_we(2, 2, 4)
+        round_we(2, 0, 2)
         quant_we(1, 2, 4)
         quant_we(1, 0, 2)
-        c_pass(1, 1, 2)
-        c_pass(1, 1, 3)
-        forecast(0, 2, 2)
-        forecast(0, 3, 3, 2)
+        e_close(0, e0)
+        e_close(1, e1)
+        damp_m(3, m3)
+        root(4)
+        copy_m(4, m4)
         round_wa_gpsimd()
-        root(1, 0)
-        damp_m_aside(1, 0, m_sum(1, 0, 0))
-        root(1, 1)
-        m11 = m_sum(1, 1, 4)
-        damp_m_aside(1, 1, m11, slice(SHARE, HALF))
-        square(1, 2)
-        square(1, 3)
-        root(1, 2)
-        root(1, 3, slice(0, 256))
-        root(1, 3, slice(256, 512))
+        damp_m_aside(4)
+        root(5)
+        copy_m(5, m5, slice(0, SHARE))
+        damp_m_aside(5, slice(0, SHARE))
+        square(6)
+        e2 = exposure(2, 2)
+        e3 = exposure(3, 3)
+        c_pass(0, 7)
+        c_pass(1, 7)
+        square(7)
+        root(6)
+        m6 = m_sum(6, 6)
+        e4 = exposure(4, 4)
+        copy_m(6, m6)
+        root(7)
         round_wa_scalar()
-        contribute(0, exposure(0, 1, True))
-        contribute(1, exposure(1, 5))
-        contribute(2, exposure(2, 2))
-        contribute(3, exposure(3, 3))
-        damp_m(1, 1, m11, slice(0, SHARE))
+        contribute(0, e0)
+        contribute(1, e1)
+        contribute(2, e2)
+        contribute(3, e3)
+        damp_m(5, m5, slice(SHARE, BANK))
+        e5 = exposure(5, 7)
+        m7 = m_sum(7, 0)
         quant_wa(0)
-        quant_h(0, 4)
-        allocate_half(0, 0)
-        forecast(1, 2, 1)
-        forecast(1, 3, 5, 2)
-        quant_wa(1)
-        allocate_half(1, 6)
-        store(0, 4)
-        e4 = exposure(4, 2)
+        quant_h(0, BANK)
+        damp_m_aside(6)
+        allocate(0, BANK, 1, (0,))
+        store(0, BANK, slice(0, 1))
         contribute(4, e4)
-        e5 = exposure(5, 3)
         contribute(5, e5)
-        quant_h(4, 1)
-        e6 = exposure(6, 7)
-        allocate(4, 1, 1)
-        contribute(6, e6)
-        quant_h(5, 1)
-        e7 = exposure(7, 2)
-        allocate(5, 1, 5)
-        store(4, 2)
+        damp_m(7, m7)
+        quant_wa(1)
+        quant_h(4 * TOK, 2 * TOK)
+        allocate(0, BANK, 5, (1,))
+        store(0, BANK, slice(1, 2))
+        allocate(4 * TOK, 2 * TOK, 6)
+        store(4 * TOK, 2 * TOK)
+        contribute(6, exposure(6, 2))
+        e7 = exposure(7, 3)
         contribute(7, e7, 0, TOK // 2)
-        quant_h(6, 1)
-        allocate(6, 1, 4)
-        store(6, 1)
+        quant_h(6 * TOK, TOK)
+        allocate(6 * TOK, TOK, 4)
+        store(6 * TOK, TOK)
         contribute(7, e7, TOK // 2, TOK // 2)
-        quant_h(7, 0.5)
-        allocate(7, 0.5, 3)
-        quant_h(7.5, 0.5)
-        allocate(7.5, 0.5, 0, nc.vector.tensor_copy)
-        store(7, 1)
+        quant_h(7 * TOK, TOK // 2)
+        allocate(7 * TOK, TOK // 2, 7)
+        quant_h(7 * TOK + TOK // 2, TOK // 2)
+        allocate(7 * TOK + TOK // 2, TOK // 2, 0, copy=nc.vector.tensor_copy)
+        store(7 * TOK, TOK)

@@ -21,9 +21,8 @@ PASSES = 2
 BANK = 512
 QUART = 256
 TOK = 128
-EARLY = 1536
-ASIDE = (4, 5, 6)
-SHARE = 256
+EARLY = 1024
+ASIDE = (4, 6)
 
 
 def tile_list_factor_risk_allocation_kernel(
@@ -106,7 +105,7 @@ def tile_list_factor_risk_allocation_kernel(
                 in_=wv_raw[a][:].bitcast(dtype).rearrange("p (g t i) -> p t g i", t=4, i=4)[:, lo:hi],
             )
 
-        c_acc = [psum.tile([P, 2, QUART], F32, name="c%d" % k, tag="bank%d" % (k % 7)) for k in range(8)]
+        c_acc = [psum.tile([P, 2, QUART], F32, name="c%d" % k, tag="bank%d" % k) for k in range(7)]
 
         def c_pass(a, k):
             q, h = divmod(k, 2)
@@ -143,11 +142,11 @@ def tile_list_factor_risk_allocation_kernel(
         m_sb = {k: keep.tile([P, BANK], F32, name="m_sb%d" % k, tag="m_sb%d" % k, align_bytes=256) for k in ASIDE}
         we_q = [keep.tile([P, H], U32, name="we_q%d" % a, align_bytes=256) for a in range(PASSES)]
         we_s = [keep.tile([P, H], U8, name="we_s%d" % a, align_bytes=256) for a in range(PASSES)]
-        wa_q = [keep.tile([P, P], U32, name="wa_q%d" % u, tag=tag, align_bytes=256) for u, tag in enumerate(("wa_q0", "damp6"))]
+        wa_q = [keep.tile([P, P], U32, name="wa_q%d" % u, tag=tag, align_bytes=256) for u, tag in enumerate(("wa_q0", "wa_q1"))]
         wa_s = keep.tile([P, N], U8, name="wa_s", align_bytes=256)
         h_q = [keep.tile([P, BANK], U32, name="h_q%d" % b, tag=tag, align_bytes=256) for b, tag in enumerate(("h_q0", "m_sb6"))]
         h_s = keep.tile([P, S], U8, name="h_s", align_bytes=256)
-        wa_bf = [keep.tile([P, P, 4], BF16, name="wa_bf%d" % u, tag=tag, align_bytes=256) for u, tag in enumerate(("we_bf1", "sq7"))]
+        wa_bf = [keep.tile([P, P, 4], BF16, name="wa_bf%d" % u, tag=tag, align_bytes=256) for u, tag in enumerate(("we_bf1", "sq5"))]
         res = keep.tile([P, 2, S], F32, name="res", align_bytes=256)
         out_v = out.rearrange("(u p) j -> p u j", p=P)
 
@@ -285,8 +284,9 @@ def tile_list_factor_risk_allocation_kernel(
         permute_wv(1, nc.scalar.copy, U32, 2, 4)
         permute_wr(0, 2)
         permute_wr(2, 4)
-        for q in range(4):
-            gather(1, QUART * q, QUART)
+        gather(1, 0, QUART)
+        gather(1, QUART, QUART)
+        gather(1, BANK, BANK)
         round_we(0, 0, 4)
         c_pass(1, 0)
         for j in range(2):
@@ -320,64 +320,63 @@ def tile_list_factor_risk_allocation_kernel(
         e0 = e_open(0, 7)
         e1 = e_open(1, 1)
         m4 = m_sum(4, 4)
-        m5 = m_sum(5, 5)
+        c_acc.append(psum.tile([P, 2, QUART], F32, name="c7", tag="bank0"))
+        c_pass(0, 7)
+        c_pass(1, 7)
+        e2 = e_open(2, 2)
         root(3)
         round_we(2, 2, 4)
         round_we(2, 0, 2)
         quant_we(1, 2, 4)
         quant_we(1, 0, 2)
-        e_close(0, e0)
-        e_close(1, e1)
+        for s, acc in enumerate((e0, e1, e2)):
+            e_close(s, acc)
         damp_m(3, m3)
+        e3 = exposure(3, 3)
         root(4)
         copy_m(4, m4)
         round_wa_gpsimd()
         damp_m_aside(4)
         root(5)
-        copy_m(5, m5, slice(0, SHARE))
-        damp_m_aside(5, slice(0, SHARE))
         square(6)
-        e2 = exposure(2, 2)
-        e3 = exposure(3, 3)
-        c_pass(0, 7)
-        c_pass(1, 7)
-        square(7)
-        root(6)
-        m6 = m_sum(6, 6)
-        e4 = exposure(4, 4)
-        copy_m(6, m6)
-        root(7)
         round_wa_scalar()
+        root(6)
+        square(7)
         contribute(0, e0)
+        m5 = m_sum(5, 7)
+        m6 = m_sum(6, 6)
+        copy_m(6, m6)
         contribute(1, e1)
+        root(7)
+        e4 = exposure(4, 4)
+        m7 = m_sum(7, 0)
+        e5 = exposure(5, 5)
         contribute(2, e2)
         contribute(3, e3)
-        damp_m(5, m5, slice(SHARE, BANK))
-        e5 = exposure(5, 7)
-        m7 = m_sum(7, 0)
+        damp_m(5, m5)
         quant_wa(0)
+        quant_wa(1)
         quant_h(0, BANK)
         damp_m_aside(6)
         allocate(0, BANK, 1, (0,))
-        store(0, BANK, slice(0, 1))
+        allocate(0, BANK, 7, (1,))
+        store(0, BANK)
         contribute(4, e4)
         contribute(5, e5)
         damp_m(7, m7)
-        quant_wa(1)
         quant_h(4 * TOK, 2 * TOK)
-        allocate(0, BANK, 5, (1,))
-        store(0, BANK, slice(1, 2))
+        e6 = exposure(6, 2)
+        e7 = exposure(7, 3)
         allocate(4 * TOK, 2 * TOK, 6)
         store(4 * TOK, 2 * TOK)
-        contribute(6, exposure(6, 2))
-        e7 = exposure(7, 3)
+        contribute(6, e6)
         contribute(7, e7, 0, TOK // 2)
         quant_h(6 * TOK, TOK)
         allocate(6 * TOK, TOK, 4)
         store(6 * TOK, TOK)
         contribute(7, e7, TOK // 2, TOK // 2)
         quant_h(7 * TOK, TOK // 2)
-        allocate(7 * TOK, TOK // 2, 7)
+        allocate(7 * TOK, TOK // 2, 5)
         quant_h(7 * TOK + TOK // 2, TOK // 2)
         allocate(7 * TOK + TOK // 2, TOK // 2, 0, copy=nc.vector.tensor_copy)
         store(7 * TOK, TOK)

@@ -134,19 +134,18 @@ def tile_list_factor_risk_allocation_kernel(
             nc.sync.dma_start(wa_raw[:, t, :], wa_rows[t])
 
         sq = [keep.tile([P, BANK], F32, name="sq%d" % k, tag="sq%d" % k, align_bytes=256) for k in range(8)]
-        damp = [[keep.tile([P, QUART], F32, name="damp%d%d" % (k, j), tag="damp%d%d" % (k, j), align_bytes=256) for j in range(2)] for k in range(1)]
-        damp = damp + [keep.tile([P, BANK], F32, name="damp%d" % k, tag="damp%d" % k, align_bytes=256) for k in range(1, 8)]
+        damp = [keep.tile([P, BANK], F32, name="damp%d" % k, align_bytes=256) for k in range(8)]
         we_bf = [keep.tile([P, 4, P, 4], BF16, name="we_bf%d" % a, tag="we_bf%d" % a, align_bytes=256) for a in range(PASSES)]
         h_bf = [keep.tile([P, BANK, 4], BF16, name="h_bf%d" % b, tag="h_bf%d" % b, align_bytes=256) for b in range(2)]
         md = [keep.tile([P, 4 * QUART], F32, name="md%d" % q, tag=tag, align_bytes=256)[:] for q, tag in enumerate(("md0", "md1", "md2", "h_bf0"))]
         m_sb = {k: keep.tile([P, BANK], F32, name="m_sb%d" % k, tag="m_sb%d" % k, align_bytes=256) for k in ASIDE}
         we_q = [keep.tile([P, H], U32, name="we_q%d" % a, align_bytes=256) for a in range(PASSES)]
         we_s = [keep.tile([P, H], U8, name="we_s%d" % a, align_bytes=256) for a in range(PASSES)]
-        wa_q = [keep.tile([P, P], U32, name="wa_q%d" % u, tag=tag, align_bytes=256) for u, tag in enumerate(("wa_q0", "wa_q1"))]
+        wa_q = keep.tile([P, N], U32, name="wa_q", align_bytes=256)
         wa_s = keep.tile([P, N], U8, name="wa_s", align_bytes=256)
         h_q = [keep.tile([P, BANK], U32, name="h_q%d" % b, tag=tag, align_bytes=256) for b, tag in enumerate(("h_q0", "m_sb6"))]
         h_s = keep.tile([P, S], U8, name="h_s", align_bytes=256)
-        wa_bf = [keep.tile([P, P, 4], BF16, name="wa_bf%d" % u, tag=tag, align_bytes=256) for u, tag in enumerate(("we_bf1", "sq5"))]
+        wa_bf = keep.tile([P, N, 4], BF16, name="wa_bf", tag="we_bf1", align_bytes=256)
         res = keep.tile([P, 2, S], F32, name="res", align_bytes=256)
         out_v = out.rearrange("(u p) j -> p u j", p=P)
 
@@ -206,19 +205,18 @@ def tile_list_factor_risk_allocation_kernel(
 
         def round_wa_gpsimd():
             nc.gpsimd.tensor_scalar(
-                out=wa_bf[0][:], in0=wa_raw[:, :, 0:P].rearrange("p t n -> p n t"),
+                out=wa_bf[:, 0:P, :], in0=wa_raw[:, :, 0:P].rearrange("p t n -> p n t"),
                 scalar1=1.0, scalar2=0.0, op0=ALU.mult, op1=ALU.add,
             )
 
         def round_wa_scalar():
             nc.scalar.copy(
-                out=wa_bf[1][:].rearrange("p (c i) t -> p c t i", i=4),
+                out=wa_bf[:, P:N, :].rearrange("p (c i) t -> p c t i", i=4),
                 in_=wa_raw[:, :, P:N].rearrange("p t (c i) -> p c t i", i=4),
             )
 
-        def quant_wa(u):
-            cols = slice(P * u, P * (u + 1))
-            nc.vector.quantize_mx(out=wa_q[u][:].bitcast(FP8X4), scales=wa_s[:, cols], in_=wa_bf[u][:].rearrange("p n t -> p (n t)"))
+        def quant_wa():
+            nc.vector.quantize_mx(out=wa_q[:].bitcast(FP8X4), scales=wa_s[:], in_=wa_bf[:].rearrange("p n t -> p (n t)"))
 
         def e_tile(s, bank):
             return psum.tile([P, 4, TOK], F32, name="e%d" % s, tag="bank%d" % bank)
@@ -268,7 +266,7 @@ def tile_list_factor_risk_allocation_kernel(
             acc = psum.tile([P, len(rows), count], F32, name="o%d_%d" % (first, rows[0]), tag="bank%d" % bank)
             for j, u in enumerate(rows):
                 nc.tensor.matmul_mx(
-                    out=acc[:, j, :], lhsT=wa_q[u][:].bitcast(FP8X4),
+                    out=acc[:, j, :], lhsT=wa_q[:, P * u : P * (u + 1)].bitcast(FP8X4),
                     lhsT_scale=wa_s[:, P * u : P * (u + 1)],
                     rhs=h_q[b][:, at : at + count].bitcast(FP8X4), rhs_scale=h_s[:, cols], start=True, stop=True,
                 )
@@ -292,10 +290,8 @@ def tile_list_factor_risk_allocation_kernel(
         for j in range(2):
             square(0, slice(QUART * j, QUART * (j + 1)))
         for j in range(2):
-            nc.scalar.activation(out=damp[0][j][:], in_=sq[0][:, QUART * j : QUART * (j + 1)], func=ACT.Abs_reciprocal_sqrt, bias=1.0)
-        m0 = m_sum(0, 7)
-        for j in range(2):
-            nc.vector.tensor_tensor(out=md[0][:, QUART * j : QUART * (j + 1)], in0=m0[:, j, :], in1=damp[0][j][:], op=ALU.mult)
+            root(0, slice(QUART * j, QUART * (j + 1)))
+        damp_m(0, m_sum(0, 7))
         c_pass(1, 1)
         c_pass(1, 2)
         square(1)
@@ -354,8 +350,7 @@ def tile_list_factor_risk_allocation_kernel(
         contribute(2, e2)
         contribute(3, e3)
         damp_m(5, m5)
-        quant_wa(0)
-        quant_wa(1)
+        quant_wa()
         quant_h(0, BANK)
         damp_m_aside(6)
         allocate(0, BANK, 1, (0,))
@@ -378,5 +373,6 @@ def tile_list_factor_risk_allocation_kernel(
         quant_h(7 * TOK, TOK // 2)
         allocate(7 * TOK, TOK // 2, 5)
         quant_h(7 * TOK + TOK // 2, TOK // 2)
-        allocate(7 * TOK + TOK // 2, TOK // 2, 0, copy=nc.vector.tensor_copy)
+        allocate(7 * TOK + TOK // 2, TOK // 2, 0, (0,), copy=nc.vector.tensor_copy)
+        allocate(7 * TOK + TOK // 2, TOK // 2, 1, (1,))
         store(7 * TOK, TOK)

from contextlib import ExitStack

import concourse.mybir as mybir

K, T, S, H, N = 1024, 4096, 1024, 512, 256
FLOPS = 2 * 3 * K * H * S + 2 * H * N * S

F32 = mybir.dt.float32
BF16 = mybir.dt.bfloat16
I32 = mybir.dt.int32
U32 = mybir.dt.uint32
U16 = mybir.dt.uint16
U8 = mybir.dt.uint8
FP8X4 = mybir.dt.float8_e4m3fn_x4
FP4X4 = mybir.dt.float4_e2m1fn_x4
ACT = mybir.ActivationFunctionType
ALU = mybir.AluOpType

P = 128
PASSES = 2
BANK = 512
QUART = 256
TOK = 128
EARLY = 1024
ASIDE = (4, 6)


def tile_list_factor_risk_allocation_kernel(
    tc, tab_words, tab_scales, offs, we, wr_words, wr_scales, wv_words, wv_scales, wa, out
):
    nc = tc.nc

    with ExitStack() as ctx:
        keep = ctx.enter_context(tc.tile_pool(name="keep", bufs=1))
        psum = ctx.enter_context(tc.psum_pool(name="psum", bufs=1))

        offsets = keep.tile([P, S // 16], U16, name="offsets")

        warm = keep.tile([P, 2], F32, name="warm")
        nc.vector.memset(warm[:, 0:1], 1.0)
        nc.scalar.activation(out=warm[:, 1:2], in_=warm[:, 0:1], func=ACT.Abs_reciprocal_sqrt)

        tsc = keep.tile([P, T // 4], I32, name="tsc", align_bytes=256)
        wsc_v = keep.tile([32, H // 4], I32, name="wsc_v", align_bytes=256)
        wsc_r = keep.tile([P, PASSES, H // 4], I32, name="wsc_r", align_bytes=256)
        nc.vector.memset(tsc[32:64, :], 0)
        nc.vector.memset(tsc[64:128, :], 0)
        nc.sync.dma_start(tsc[0:32, :], tab_scales.rearrange("a q t -> q a t").bitcast(I32))
        nc.sync.dma_start(offsets[:], offs)
        nc.sync.dma_start(wsc_v[:], wv_scales.rearrange("a q y -> q a y").bitcast(I32))

        wv_raw = [keep.tile([P, H], I32, name="wv_raw%d" % a, align_bytes=256) for a in range(PASSES)]
        nc.sync.dma_start(wv_raw[0][:], wv_words[0].rearrange("p y i -> p (y i)").bitcast(I32))
        tab0 = keep.tile([P, T], I32, name="tab0", align_bytes=256)
        nc.sync.dma_start(tab0[:], tab_words[0].rearrange("p t i -> p (t i)").bitcast(I32))
        tab1 = keep.tile([P, T], I32, name="tab1", align_bytes=256)
        tab1_words = tab_words[1].rearrange("p t i -> p (t i)").bitcast(I32)
        nc.sync.dma_start(tab1[:, 0:EARLY], tab1_words[:, 0:EARLY])

        PW = (S + H) // 4
        planes = keep.tile([P, PASSES, PW], I32, name="planes", align_bytes=256)
        nc.vector.memset(planes[:], 0)
        nc.gpsimd.memset(wsc_r[:], 0)
        for q in (0, 2, 1, 3):
            rows = wr_scales[:, 4 * q : 4 * q + 4, :].rearrange("a r y -> r a y").bitcast(I32)
            nc.gpsimd.dma_start(wsc_r[32 * q : 32 * q + 4], rows)
        wr_s = keep.tile([P, PASSES, H // 4], I32, name="wr_s", align_bytes=256)
        nc.gpsimd.tensor_copy(
            out=wr_s[:].rearrange("p a (t g) -> p a t g", t=4), in_=wsc_r[:].rearrange("p a (g t) -> p a t g", t=4)
        )
        sg = keep.tile([P, S], U8, name="sg", align_bytes=256)
        nc.vector.tensor_copy(sg[:], tsc[:].bitcast(U8).indirect(offsets[:]))
        stage = keep.tile([32, PW], I32, name="stage", align_bytes=256)
        nc.vector.tensor_copy(
            out=stage[:, S // 4 : PW].rearrange("p (t c k) -> p c t k", t=4, k=4),
            in_=wsc_v[:].rearrange("p (c k t) -> p c t k", t=4, k=4),
        )
        nc.vector.tensor_copy(out=stage[:, 0 : S // 4], in_=sg[0:32, :].bitcast(I32))
        for q in (0, 2, 1, 3):
            nc.sync.dma_start(planes[32 * q : 32 * q + 4, :, :], stage[8 * q : 8 * q + 8, :])
        nc.sync.dma_start(tab1[:, EARLY:T], tab1_words[:, EARLY:T])
        planes8 = planes[:].bitcast(U8)

        def v_scale(a, lo, n):
            return planes8[:, a, lo : lo + n]

        def wv_scale(a, t):
            return planes8[:, a, S + P * t : S + P * (t + 1)]

        def wr_scale(a, t):
            return wr_s[:].bitcast(U8)[:, a, P * t : P * (t + 1)]

        vq = [keep.tile([P, S], U32, name="vq%d" % a, align_bytes=256) for a in range(PASSES)]

        def gather(a, lo, n):
            win = (tab0[:], tab1[:])[a]
            nc.vector.tensor_copy(vq[a][:, lo : lo + n], win.bitcast(U32).indirect(offsets[:, lo // 16 : (lo + n) // 16]))

        wv_q = [keep.tile([P, H], I32, name="wv_q%d" % a, align_bytes=256) for a in range(PASSES)]
        wr_q = keep.tile([P, PASSES, H // 2], I32, name="wr_q", align_bytes=256)

        def permute_wv(a, copy, dtype, lo, hi):
            copy(
                out=wv_q[a][:].bitcast(dtype).rearrange("p (t g i) -> p t g i", t=4, i=4)[:, lo:hi],
                in_=wv_raw[a][:].bitcast(dtype).rearrange("p (g t i) -> p t g i", t=4, i=4)[:, lo:hi],
            )

        c_acc = [psum.tile([P, 2, QUART], F32, name="c%d" % k, tag="bank%d" % k) for k in range(7)]

        def c_pass(a, k):
            q, h = divmod(k, 2)
            for j in range(2):
                t = 2 * h + j
                nc.tensor.matmul_mx(
                    out=c_acc[k][:, j, :], lhsT=wv_q[a][:, P * t : P * (t + 1)].bitcast(FP8X4), lhsT_scale=wv_scale(a, t),
                    rhs=vq[a][:, QUART * q : QUART * (q + 1)].bitcast(FP8X4), rhs_scale=v_scale(a, QUART * q, QUART),
                    start=(a, j) == (0, 0), stop=(a, j) == (1, 1),
                )

        gather(0, 0, BANK)
        gather(0, BANK, BANK)
        permute_wv(0, nc.vector.tensor_copy, I32, 0, 4)

        wr_raw = keep.tile([P, PASSES, H // 2], I32, name="wr_raw", align_bytes=256)
        we_parts = ((0, 0, H // 2), (0, H // 2, H), (1, 0, H))
        we_raw = [keep.tile([P, 4, hi - lo], F32, name="we_raw%d" % i, align_bytes=256) for i, (a, lo, hi) in enumerate(we_parts)]
        wa_raw = keep.tile([P, 4, N], F32, name="wa_raw", align_bytes=256)
        nc.sync.dma_start(wv_raw[1][:], wv_words[1].rearrange("p y i -> p (y i)").bitcast(I32))
        nc.sync.dma_start(wr_raw[:], wr_words.rearrange("a p y -> p a y").bitcast(I32))
        for raw, (a, lo, hi) in zip(we_raw, we_parts):
            nc.sync.dma_start(raw[:], we[512 * a : 512 * (a + 1), lo:hi].rearrange("(p j) r -> p j r", j=4))
        wa_rows = wa.rearrange("(g t i) n -> t g i n", t=4, i=4)
        for t in range(4):
            nc.sync.dma_start(wa_raw[:, t, :], wa_rows[t])

        sq = [keep.tile([P, BANK], F32, name="sq%d" % k, tag="sq%d" % k, align_bytes=256) for k in range(8)]
        damp = [keep.tile([P, BANK], F32, name="damp%d" % k, align_bytes=256) for k in range(8)]
        we_bf = [keep.tile([P, 4, P, 4], BF16, name="we_bf%d" % a, tag="we_bf%d" % a, align_bytes=256) for a in range(PASSES)]
        h_bf = [keep.tile([P, BANK, 4], BF16, name="h_bf%d" % b, tag="h_bf%d" % b, align_bytes=256) for b in range(2)]
        md = [keep.tile([P, 4 * QUART], F32, name="md%d" % q, tag=tag, align_bytes=256)[:] for q, tag in enumerate(("md0", "md1", "md2", "h_bf0"))]
        m_sb = {k: keep.tile([P, BANK], F32, name="m_sb%d" % k, tag="m_sb%d" % k, align_bytes=256) for k in ASIDE}
        we_q = [keep.tile([P, H], U32, name="we_q%d" % a, align_bytes=256) for a in range(PASSES)]
        we_s = [keep.tile([P, H], U8, name="we_s%d" % a, align_bytes=256) for a in range(PASSES)]
        wa_q = keep.tile([P, N], U32, name="wa_q", align_bytes=256)
        wa_s = keep.tile([P, N], U8, name="wa_s", align_bytes=256)
        h_q = [keep.tile([P, BANK], U32, name="h_q%d" % b, tag=tag, align_bytes=256) for b, tag in enumerate(("h_q0", "m_sb6"))]
        h_s = keep.tile([P, S], U8, name="h_s", align_bytes=256)
        wa_bf = keep.tile([P, N, 4], BF16, name="wa_bf", tag="we_bf1", align_bytes=256)
        res = keep.tile([P, 2, S], F32, name="res", align_bytes=256)
        out_v = out.rearrange("(u p) j -> p u j", p=P)

        def permute_wr(lo, hi):
            nc.gpsimd.tensor_copy(
                out=wr_q[:].rearrange("p a (t g i) -> p a t g i", t=4, i=2)[:, :, lo:hi],
                in_=wr_raw[:].rearrange("p a (g t i) -> p a t g i", t=4, i=2)[:, :, lo:hi],
            )

        def flat(acc):
            return acc[:].rearrange("p j n -> p (j n)")

        def square(k, cols=slice(0, BANK)):
            nc.scalar.activation(out=sq[k][:, cols], in_=flat(c_acc[k])[:, cols], func=ACT.Square)

        def root(k, cols=slice(0, BANK)):
            nc.scalar.activation(out=damp[k][:, cols], in_=sq[k][:, cols], func=ACT.Abs_reciprocal_sqrt, bias=1.0)

        def m_sum(k, bank):
            q, h = divmod(k, 2)
            acc = psum.tile([P, 2, QUART], F32, name="m%d" % k, tag="bank%d" % bank)
            for j in range(2):
                t = 2 * h + j
                for a in range(PASSES):
                    nc.tensor.matmul_mx(
                        out=acc[:, j, :], lhsT=wr_q[:, a, 64 * t : 64 * (t + 1)].bitcast(U8).bitcast(FP4X4), lhsT_scale=wr_scale(a, t),
                        rhs=vq[a][:, QUART * q : QUART * (q + 1)].bitcast(FP8X4), rhs_scale=v_scale(a, QUART * q, QUART),
                        start=(a == 0), stop=(a == 1),
                    )
            return acc

        def md_of(k):
            q, h = divmod(k, 2)
            return md[q][:, BANK * h : BANK * (h + 1)]

        def damp_m(k, acc, cols=slice(0, BANK)):
            nc.vector.tensor_tensor(out=md_of(k)[:, cols], in0=flat(acc)[:, cols], in1=damp[k][:, cols], op=ALU.mult)

        def copy_m(k, acc, cols=slice(0, BANK)):
            nc.scalar.copy(out=m_sb[k][:, cols], in_=flat(acc)[:, cols])

        def damp_m_aside(k, cols=slice(0, BANK)):
            nc.gpsimd.tensor_tensor(out=md_of(k)[:, cols], in0=m_sb[k][:, cols], in1=damp[k][:, cols], op=ALU.mult)

        def round_we(part, lo, hi):
            a, first, last = we_parts[part]
            dst = we_bf[a][:, lo:hi, first // 4 : last // 4, :].rearrange("p t (g i) j -> p t g j i", i=4)
            src = we_raw[part][:].rearrange("p j (g t i) -> p t g j i", t=4, i=4)[:, lo:hi]
            nc.vector.tensor_copy(out=dst, in_=src)

        def quant_we(a, lo, hi):
            cols = slice(P * lo, P * hi)
            nc.vector.quantize_mx(
                out=we_q[a][:, cols].bitcast(FP8X4), scales=we_s[a][:, cols],
                in_=we_bf[a][:, lo:hi].rearrange("p t c j -> p (t c j)"),
            )

        def round_wa_gpsimd():
            nc.gpsimd.tensor_scalar(
                out=wa_bf[:, 0:P, :], in0=wa_raw[:, :, 0:P].rearrange("p t n -> p n t"),
                scalar1=1.0, scalar2=0.0, op0=ALU.mult, op1=ALU.add,
            )

        def round_wa_scalar():
            nc.scalar.copy(
                out=wa_bf[:, P:N, :].rearrange("p (c i) t -> p c t i", i=4),
                in_=wa_raw[:, :, P:N].rearrange("p t (c i) -> p c t i", i=4),
            )

        def quant_wa():
            nc.vector.quantize_mx(out=wa_q[:].bitcast(FP8X4), scales=wa_s[:], in_=wa_bf[:].rearrange("p n t -> p (n t)"))

        def e_tile(s, bank):
            return psum.tile([P, 4, TOK], F32, name="e%d" % s, tag="bank%d" % bank)

        def e_passes(s, acc, steps):
            cols = slice(TOK * s, TOK * (s + 1))
            for t, a, start, stop in steps:
                nc.tensor.matmul_mx(
                    out=acc[:, t, :], lhsT=we_q[a][:, P * t : P * (t + 1)].bitcast(FP8X4),
                    lhsT_scale=we_s[a][:, P * t : P * (t + 1)],
                    rhs=vq[a][:, cols].bitcast(FP8X4), rhs_scale=v_scale(a, TOK * s, TOK), start=start, stop=stop,
                )

        def e_open(s, bank):
            acc = e_tile(s, bank)
            e_passes(s, acc, [(t, 0, t == 0, False) for t in range(4)])
            return acc

        def e_close(s, acc):
            e_passes(s, acc, [(t, 1, False, t == 1) for t in (2, 3, 0, 1)])

        def exposure(s, bank):
            acc = e_tile(s, bank)
            e_passes(s, acc, [(t, a, a == 1, a == 0) for t in (2, 3, 0, 1) for a in (1, 0)])
            return acc

        def contribute(s, acc, first=0, count=TOK):
            q, lo = divmod(TOK * s + first, QUART)
            b, at = divmod(TOK * s + first, BANK)
            nc.vector.tensor_tensor(
                out=h_bf[b][:, at : at + count, :].rearrange("p (c i) t -> p c t i", i=4),
                in0=acc[:, :, first : first + count].rearrange("p t (c i) -> p c t i", i=4),
                in1=md[q].rearrange("p (t n) -> p t n", t=4)[:, :, lo : lo + count].rearrange("p t (c i) -> p c t i", i=4),
                op=ALU.mult,
            )

        def quant_h(first, count):
            b, at = divmod(first, BANK)
            nc.vector.quantize_mx(
                out=h_q[b][:, at : at + count].bitcast(FP8X4), scales=h_s[:, first : first + count],
                in_=h_bf[b][:, at : at + count, :].rearrange("p n t -> p (n t)"),
            )

        def allocate(first, count, bank, rows=(0, 1), copy=nc.scalar.copy):
            cols = slice(first, first + count)
            b, at = divmod(first, BANK)
            acc = psum.tile([P, len(rows), count], F32, name="o%d_%d" % (first, rows[0]), tag="bank%d" % bank)
            for j, u in enumerate(rows):
                nc.tensor.matmul_mx(
                    out=acc[:, j, :], lhsT=wa_q[:, P * u : P * (u + 1)].bitcast(FP8X4),
                    lhsT_scale=wa_s[:, P * u : P * (u + 1)],
                    rhs=h_q[b][:, at : at + count].bitcast(FP8X4), rhs_scale=h_s[:, cols], start=True, stop=True,
                )
            copy(out=res[:, rows[0] : rows[-1] + 1, cols], in_=acc[:])

        def store(first, count, rows=slice(0, 2)):
            cols = slice(first, first + count)
            nc.sync.dma_start(out_v[:, rows, cols], res[:, rows, cols])

        for k in range(7):
            c_pass(0, k)
        permute_wv(1, nc.scalar.copy, U32, 0, 2)
        permute_wv(1, nc.scalar.copy, U32, 2, 4)
        permute_wr(0, 2)
        permute_wr(2, 4)
        gather(1, 0, QUART)
        gather(1, QUART, QUART)
        gather(1, BANK, BANK)
        round_we(0, 0, 4)
        c_pass(1, 0)
        for j in range(2):
            square(0, slice(QUART * j, QUART * (j + 1)))
        for j in range(2):
            root(0, slice(QUART * j, QUART * (j + 1)))
        damp_m(0, m_sum(0, 7))
        c_pass(1, 1)
        c_pass(1, 2)
        square(1)
        m1 = m_sum(1, 1)
        square(2)
        m2 = m_sum(2, 2)
        c_pass(1, 3)
        root(1)
        root(2)
        round_we(1, 0, 2)
        round_we(1, 2, 4)
        quant_we(0, 0, 2)
        quant_we(0, 2, 4)
        damp_m(1, m1)
        damp_m(2, m2)
        for k in range(4, 7):
            c_pass(1, k)
        square(3)
        m3 = m_sum(3, 3)
        square(4)
        square(5)
        e0 = e_open(0, 7)
        e1 = e_open(1, 1)
        m4 = m_sum(4, 4)
        c_acc.append(psum.tile([P, 2, QUART], F32, name="c7", tag="bank0"))
        c_pass(0, 7)
        c_pass(1, 7)
        e2 = e_open(2, 2)
        root(3)
        round_we(2, 2, 4)
        round_we(2, 0, 2)
        quant_we(1, 2, 4)
        quant_we(1, 0, 2)
        for s, acc in enumerate((e0, e1, e2)):
            e_close(s, acc)
        damp_m(3, m3)
        e3 = exposure(3, 3)
        root(4)
        copy_m(4, m4)
        round_wa_gpsimd()
        damp_m_aside(4)
        root(5)
        square(6)
        round_wa_scalar()
        root(6)
        square(7)
        contribute(0, e0)
        m5 = m_sum(5, 7)
        m6 = m_sum(6, 6)
        copy_m(6, m6)
        contribute(1, e1)
        root(7)
        e4 = exposure(4, 4)
        m7 = m_sum(7, 0)
        e5 = exposure(5, 5)
        contribute(2, e2)
        contribute(3, e3)
        damp_m(5, m5)
        quant_wa()
        quant_h(0, BANK)
        damp_m_aside(6)
        allocate(0, BANK, 1, (0,))
        allocate(0, BANK, 7, (1,))
        store(0, BANK)
        contribute(4, e4)
        contribute(5, e5)
        damp_m(7, m7)
        quant_h(4 * TOK, 2 * TOK)
        e6 = exposure(6, 2)
        e7 = exposure(7, 3)
        allocate(4 * TOK, 2 * TOK, 6)
        store(4 * TOK, 2 * TOK)
        contribute(6, e6)
        contribute(7, e7, 0, TOK // 2)
        quant_h(6 * TOK, TOK)
        allocate(6 * TOK, TOK, 4)
        store(6 * TOK, TOK)
        contribute(7, e7, TOK // 2, TOK // 2)
        quant_h(7 * TOK, TOK // 2)
        allocate(7 * TOK, TOK // 2, 5)
        quant_h(7 * TOK + TOK // 2, TOK // 2)
        allocate(7 * TOK + TOK // 2, TOK // 2, 0, (0,), copy=nc.vector.tensor_copy)
        allocate(7 * TOK + TOK // 2, TOK // 2, 1, (1,))
        store(7 * TOK, TOK)
